import numpy as np, ml_dtypes
CORES = [25,29,65,69,153,157,193,197]
N = 8
import mx_ref
BF = ml_dtypes.bfloat16
def entries(a):
    return np.ascontiguousarray(a.T).reshape(-1)
def table(e):
    return np.ascontiguousarray(np.reshape(e, (-1, 16)).T).astype(np.int32)
def pick(q, e):
    c = np.concatenate([q[0].reshape(128, -1, 4), np.zeros((128, 1, 4), np.uint8)], axis=1); s = np.concatenate([q[1], np.ones((16, 1), np.uint8)], axis=1)
    return (np.ascontiguousarray(c[:, e].reshape(128, -1)), np.ascontiguousarray(s[:, e]))
def join(*qs):
    return (np.concatenate([q[0] for q in qs], axis=1), np.concatenate([q[1] for q in qs], axis=1))
def put(q, e, v):
    c, s = q[0].reshape(128, -1, 4).copy(), q[1].copy(); c[:, e] = v[0].reshape(128, -1, 4); s[:, e] = v[1]
    return (c.reshape(128, -1), s)
def pk(c, s):
    return (np.ascontiguousarray(c), mx_ref.live(s))
def emit(q):
    return q[0], q[1]
def decode(q):
    o = []
    for b in range(4):
        e = np.zeros((128, 128, 4), np.float32); e[np.arange(128), np.arange(128), b] = 1
        o.append(mx_ref.matmul(mx_ref.quantize(e.reshape(128, 512).astype(BF)), q))
    return np.stack(o, axis=2).reshape(128, -1)
def f(rng, *shape):
    return mx_ref.flush((rng.standard_normal(shape, dtype=np.float32) * np.exp2(rng.integers(-2, 3, shape[:-1] + (1,)))).astype(BF))
def wide(rng, *shape, cols=0):
    v = rng.standard_normal(shape, dtype=np.float32) * np.exp2(rng.integers(-12, 13, shape)).astype(np.float32)
    if cols: v *= np.repeat(np.exp2(rng.integers(-cols, cols + 1, shape[:-2] + (1, shape[-1] // 4))) * (rng.random(shape[:-2] + (1, shape[-1] // 4)) > 0.0625), 4, axis=-1).astype(np.float32)
    return mx_ref.flush(v.astype(BF))
M, K, J, R = 192, 48, 3, 3
def unpack(q):
    c = q[0].reshape(16, 8, -1, 4).astype(int)
    s = np.broadcast_to(q[1].astype(int)[:, None, :, None], c.shape)
    k = np.unique(q[1]).astype(int)
    k = np.concatenate([k, np.ones(4 + k.size % 2, int)])
    here = np.zeros((256, 256), np.uint8)
    here[s, c] = c
    z = np.zeros((128, k.size, 4), np.uint8)
    z[:64] = here[k].reshape(-1, 64, 4).transpose(1, 0, 2)
    v = decode((z.reshape(128, -1), np.repeat(k[None], 16, axis=0).astype(np.uint8)))
    held = np.zeros((256, 256), np.float32)
    held[k] = v.reshape(128, -1, 4)[:64].transpose(1, 0, 2).reshape(-1, 256)
    return held[s, c].reshape(128, -1)
def big(v):
    v = np.array(v)
    v[np.abs(v.astype(np.float32)) < np.float32(2.0 ** -16)] = 0
    return v
def bf(v):
    return np.asarray(v, np.float32).astype(BF)
def parts(t):
    return t.reshape(N, 128, -1, 4)
def store(e):
    return np.stack([table(v.T) for v in e.reshape(N, M, J)])
def setup_inputs(rng):
    return {"x": big(f(rng, N, 128, 4 * M)), "u": np.array(f(rng, N, 128, 512)), "w": np.array(f(rng, N, 128, 512)), "nb": store(rng.integers(0, N * M, (N * M, J)))}
def setup_inputs_chain(rng):
    d, n = setup_inputs(rng), N * M
    at = rng.permutation(n)
    e = at[rng.integers(0, np.arange(1, n + 1)[:, None], (n, J))]
    j = np.arange(n - 1)
    e[j, rng.integers(0, J, n - 1)] = at[j + 1]
    nb, h = np.zeros((n, J), int), np.zeros(n, int)
    nb[at], h[at] = e, np.arange(n)
    x, u = parts(d["x"]), parts(d["u"])
    x[:, :16] = 0
    u[:, :, :R] = 0
    for k in range(12):
        x[:, 4 * (k // 4), :, k % 4] = bf((h >> k & 1).reshape(N, M))
        u[:, 4 * (k // 4), :R, k % 4] = 2.0 ** k
    return {"x": x.reshape(N, 128, -1), "u": u.reshape(N, 128, -1), "w": d["w"], "nb": store(nb)}
def setup_inputs_deep(rng):
    d, n = setup_inputs(rng), N * M
    at = np.sort(rng.permutation(n).reshape(-1, 4), axis=1)
    nb, low = np.zeros((n, J), int), np.zeros(n)
    for k in range(4): nb[at[:, k]] = at[:, [min(k + i, 3) for i in (1, 2, 3)]]
    low[at[1::2]] = 11
    x, u = parts(d["x"]), parts(d["u"])
    u[:, :, :R] = 0
    for t, k in enumerate(rng.permutation(R)):
        v = np.zeros(n)
        v[at] = [(4, 4, 4, 7), (4, 7, 4, 6), (7, 7, 5, 5)][k]
        x[:, 40 * t:40 * t + 40] = bf((v - low).reshape(N, 1, M, 1) * 2.0 ** 27)
        u[:, 40 * t:40 * t + 40, t] = 2.0 ** 30
    return {"x": x.reshape(N, 128, -1), "u": u.reshape(N, 128, -1), "w": d["w"], "nb": store(rng.permuted(nb, axis=1))}
def setup_inputs_peaks(rng):
    d, n = setup_inputs(rng), N * M
    who = rng.permutation(N)
    peaks = [M * who[t] + rng.permutation(M)[:K] for t in range(R)]
    lone = np.zeros(n, bool)
    lone[np.concatenate(peaks)] = True
    lone[M * who[R]:M * who[R] + M] = True
    m = np.flatnonzero(~lone)
    nb = np.repeat(np.arange(n)[:, None], J, axis=1)
    x, u = parts(d["x"]), parts(d["u"])
    u[:, :, :R] = mx_ref.flush(bf(u[:, :, :R].astype(np.float32) * np.float32(2.0 ** -6)))
    for t in range(R):
        nb[m, t] = rng.permutation(np.concatenate([peaks[t], peaks[t], rng.choice(peaks[t], m.size - 2 * K)]))
        level = rng.integers(1, 4, n)
        level[peaks[t]] = 7
        x[:, 32 * t:32 * t + 16] = 0
        u[:, 32 * t:32 * t + 16, :R] = 0
        x[:, 32 * t, :, 0] = bf(level.reshape(N, M))
        u[:, 32 * t, t, 0] = 1024
    return {"x": x.reshape(N, 128, -1), "u": u.reshape(N, 128, -1), "w": d["w"], "nb": store(rng.permuted(nb, axis=1))}
def setup_inputs_spread(rng):
    return {**setup_inputs(rng), "x": big(wide(rng, N, 128, 4 * M, cols=6))}
def setup_inputs_ties(rng):
    d = setup_inputs(rng)
    x, u = parts(d["x"]), parts(d["u"])
    x[:, :16] = 0
    x[:, 0, :, 0] = 4
    u[:, :, :R] = 0
    u[:, 0, :R, 0] = -2.0 ** 30
    for t in range(R):
        p = 32 * t + 32
        x[:, p:p + 16] = 0
        x[:, p, :, 0] = bf(rng.integers(4, 8, (N, M)))
        u[:, p, t, 0] = 1024
    return {"x": x.reshape(N, 128, -1), "u": u.reshape(N, 128, -1), "w": d["w"], "nb": d["nb"]}
def check_inputs(d):
    b = []
    for k in ("x", "u", "w"):
        v = np.abs(d[k].astype(np.float32))
        if not (np.isfinite(v).all() and ((v == 0) | (v >= 2.0 ** -30) & (v <= 2.0 ** 30)).all()): b.append("a value of " + k)
    if d["nb"].min() < 0 or d["nb"].max() >= N * M: b.append("nb")
    return b
def reference(x, u, w, nb):
    node = np.arange(N * M)
    near = np.concatenate([entries(nb[r]).reshape(J, M).T for r in range(N)])
    near = np.sort(np.concatenate([node[:, None], near], axis=1), axis=1)
    state = join(*[mx_ref.quantize(np.ascontiguousarray(x[r])) for r in range(N)])
    own = node.reshape(N, M)
    pieces = [np.concatenate([own[r], np.full(-M % 128, -1)]).reshape(-1, 128) for r in range(N)]
    qu = [mx_ref.quantize(np.ascontiguousarray(u[r][:, :16])) for r in range(N)]
    y, rt = np.zeros((N, 128, M), np.float32), np.zeros((N, 1, R * M), np.float32)
    oc, osc = np.zeros((N, 128, 4 * M), np.uint8), np.zeros((N, 16, M), np.uint8)
    for t in range(R):
        h = np.concatenate([np.concatenate([mx_ref.matmul(pick(state, e), qu[r])[:, t] for e in pieces[r]])[:M] for r in range(N)]) + np.float32(0)
        root = near[node, np.argmax(h[near], axis=1)]
        while (root[root] != root).any(): root = root[root]
        size = np.bincount(root, minlength=N * M)
        chosen = np.argsort(-size, kind="stable")[:K]
        m = np.flatnonzero(np.isin(root, chosen) & (root != node))
        if m.size:
            v = unpack(state).reshape(128, N * M, 4)
            v = (v[:, m] + v[:, root[m]]) * np.float32(0.5)
            v = np.concatenate([v, np.zeros((128, -m.size % 4, 4), np.float32)], axis=1)
            new = mx_ref.quantize(np.ascontiguousarray(v.reshape(128, -1).astype(BF)))
            state = put(state, m, pick(new, np.arange(m.size)))
        rt[:, 0, t * M:t * M + M] = root.reshape(N, M)
    for r in range(N):
        y[r] = mx_ref.matmul(mx_ref.quantize(np.ascontiguousarray(w[r])), pick(state, own[r]))
        oc[r], osc[r] = emit(pick(state, own[r]))
    return {"y": y, "oc": oc, "osc": osc, "rt": rt}

@@ -1,0 +1,647 @@
+from concourse.bass import DstId, RemoteDMATransfer
+from concourse.mybir import dt, AluOpType, AxisListType, ActivationFunctionType
+
+N, M, K, J, R = 8, 192, 48, 3, 3
+NN = N * M
+LEVELS = [2, 2, 2, 0]
+TAIL = 4
+FIRST_S = 52
+WIDE_S = 64
+HAND_ENG = 4
+C4, U8, F32, B16, I32, U16 = "float8_e4m3fn_x4", "uint8", "float32", "bfloat16", "int32", "uint16"
+
+SCRATCH = {"pd": ("psum", [128, 2048], F32), "ph": ("psum", [128, 512], F32)}
+for _d, _l in (
+        (B16, (("xt", 768), ("ut", 512), ("wt", 512), ("et", 2048), ("nt", 768), ("ms", 2 * R), ("lea", 32 * R), ("leb", 8 * R),
+               ("lw", 6 * R), ("lml", 48 * R), ("rm", 2 * R), ("rl", 6 * R), ("ex", NN), ("vw", NN), ("rs32", 192),
+               ("b1", 192), ("b2", 192), ("b3", 192))),
+        (F32, (("pf", 8), ("iot", NN), ("ta", NN), ("tb", NN), ("j16", 576), ("diag", 320), ("rs16", 576), ("fw", 320),
+               ("fw2", 320), ("cw", 1696), ("sm", 832), ("hs", 6 * R), ("hl", 64 * R), ("rh", 6 * R), ("mk", 576), ("g3", 576),
+               ("g3t", 576), ("sc", 832), ("ht", 192), ("g2", 384), ("g2t", 384), ("w1", 192), ("w2", 192), ("w3", 192), ("w4", 192),
+               ("sj", 384), ("rho", 192 * R), ("yb", 192), ("gy", 96), ("gyt", 96))),
+        ("float16", (("g1", 192), ("g1t", 192))),
+        (I32, (("pi", 8), ("ci", 112), ("ni", 256), ("nbw", 36))),
+        (U16, (("ou", 704), ("nbs", 16), ("nbl", 80), ("rn", 10)))):
+    for _n, _w in _l:
+        SCRATCH[_n] = ("sbuf", [128, _w], _d)
+_mx = [("u", 128), ("ur", 384), ("w", 128), ("e", 512)] + [("on%d" % _t, 384) for _t in range(R + 1)]
+for _t in range(R):
+    _mx += [("%s%d" % (_n, _t), _w) for _n, _w in (("qa", 48), ("pa", 48), ("la", 64), ("pb", 16), ("rb", 12), ("lb", 96), ("rc", 192))]
+for _n, _w in _mx:
+    SCRATCH[_n + "q"] = ("sbuf", [128, _w], C4)
+    SCRATCH[_n + "s"] = ("sbuf", [128, _w], U8)
+
+SEMAPHORES = ["v", "x", "z", "s", "p", "c", "ls", "dx", "du", "dw", "dn", "out", "an", "rn", "on"]
+for _t in range(R):
+    for _n in ("ah", "aa", "ab", "al", "a1", "a2", "rh", "rm", "rl", "r2", "r3", "oh", "ol", "o2"):
+        SEMAPHORES.append("%s%d" % (_n, _t))
+
+A = AluOpType
+F = ActivationFunctionType
+X = AxisListType.X
+
+
+def _mask(engs):
+    m = 0
+    for e in engs:
+        m |= 1 << e
+    return m
+
+
+def _plan(T, topo):
+    cores = list(T.cores)
+    plan = []
+    for r, c in enumerate(cores):
+        near = [q for q in range(N) if q == r or topo.may_write(c, cores[q])]
+        far = [q for q in range(N) if q not in near]
+        hands = [h for h in topo.cores_of(c) if h not in cores and topo.die(h) == topo.die(c)
+                 and all(topo.may_write(h, cores[q]) for q in far)][:2]
+        per = len(far) // len(hands)
+        plan.append({"near": near, "far": far, "hands": [(h, far[k * per:(k + 1) * per]) for k, h in enumerate(hands)]})
+    return plan
+
+
+def _q(T, name, a, b):
+    return T[name + "q"][:, a:b].bitcast(dt.uint8)
+
+
+def _dst(topo, dst, src):
+    rid, pid = topo.addr(dst, src)
+    return DstId(rid=rid, pnc=pid)
+
+
+def hand_program(g, core, T, topo, plan, r, dests):
+    cores = list(T.cores)
+    j = plan[r]["near"].index(r)
+    engs = topo.engines(core, cores[dests[0]])
+    per = len(engs) // len(dests)
+    sent = [0]
+
+    def fwd(src, dst, sem):
+        g.remote_dma_fused([RemoteDMATransfer(dst_ids=[_dst(topo, cores[d], core)], dma_engine_mask=_mask(engs[k * per:(k + 1) * per]),
+                                              remote_sem=T.sem[sem], src=src, dst=dst) for k, d in enumerate(dests)], local_sem=T.sem.ls)
+        sent[0] += per * len(dests)
+
+    g.wait_ge(T.sem.rn, HAND_ENG)
+    fwd(T.rn[:, 0:10], T.nbl[:, 10 * r:10 * r + 10], "an")
+    for t in range(R):
+        g.wait_ge(T.sem["rh%d" % t], HAND_ENG)
+        fwd(T.rh[:, 6 * t:6 * t + 6], T.hl[:, 64 * t + 6 * r:64 * t + 6 * r + 6], "ah%d" % t)
+        g.wait_ge(T.sem["rm%d" % t], 2)
+        fwd(T.rm[:, 2 * t:2 * t + 2], T.leb[:, 8 * t + 2 * j:8 * t + 2 * j + 2], "ab%d" % t)
+        g.wait_ge(T.sem["rl%d" % t], HAND_ENG)
+        fwd(T.rl[:, 6 * t:6 * t + 6], T.lml[:, 48 * t + 6 * r:48 * t + 6 * r + 6], "al%d" % t)
+        g.wait_ge(T.sem["r2%d" % t], HAND_ENG)
+        fwd(_q(T, "rb%d" % t, 0, 12), _q(T, "lb%d" % t, 48 + 12 * j, 60 + 12 * j), "a2%d" % t)
+        g.wait_ge(T.sem["r3%d" % t], HAND_ENG)
+        fwd(T["rb%ds" % t][:, 0:12], T["lb%ds" % t][:, 48 + 12 * j:60 + 12 * j], "a2%d" % t)
+    g.wait_ge(T.sem.ls, sent[0])
+
+
+def rank_program(g, core, T, topo):
+    plan = _plan(T, topo)
+    rank = T.rank_of(core)
+    if rank is None:
+        for r in range(N):
+            for h, dests in plan[r]["hands"]:
+                if h == core:
+                    hand_program(g, core, T, topo, plan, r, dests)
+        return
+    cores = list(T.cores)
+    r = rank
+    near, far, hands = plan[r]["near"], plan[r]["far"], plan[r]["hands"]
+    jo = near.index(r)
+    qa = r // 2
+    V, S, P, Y = g.vector, g.scalar, g.tensor, g.sync
+    Q = {"v": V, "x": V, "z": V, "s": S, "p": P, "c": g, "y": Y}
+    cnt = {q: 0 for q in "vxzspc"}
+    force = {q: False for q in "vxzspc"}
+    waited = {}
+    total = {}
+
+    def wait(q, tok):
+        name, val = tok
+        q = "v" if q in "xz" else q
+        if val > waited.get((q, name), 0):
+            Q[q].wait_ge(T.sem[name], val)
+            waited[(q, name)] = val
+
+    def op(q, f, deps=(), free=False):
+        for d in deps:
+            wait(q, d)
+        if not free or force[q]:
+            wait(q, (q, cnt[q]))
+        force[q] = False
+        f().then_inc(T.sem[q], 1)
+        cnt[q] += 1
+
+    def tok(q):
+        force[q] = True
+        return (q, cnt[q])
+
+    def dma(q, out, in_, sem, deps=()):
+        for d in deps:
+            wait(q, d)
+        Q[q].dma_start(out, in_).then_inc(T.sem[sem], 16)
+        total[sem] = total.get(sem, 0) + 16
+        return (sem, total[sem])
+
+    def cp(out, in_, deps=(), free=False, q="v"):
+        op(q, lambda: V.tensor_copy(out, in_), deps, free)
+
+    def tt(out, a, b, o, deps=(), free=False):
+        op("v", lambda: V.tensor_tensor(out, a, b, o), deps, free)
+
+    def ts(out, a, s1, o1, s2=None, o2=None, deps=(), free=False):
+        if o2 is None:
+            op("v", lambda: V.tensor_scalar(out, a, s1, None, o1), deps, free)
+        else:
+            op("v", lambda: V.tensor_scalar(out, a, s1, s2, o1, o2), deps, free)
+
+    def tr(out, in_, deps=(), free=False, q="v"):
+        op(q, lambda: V.transpose(out, in_), deps, free)
+
+    def red(out, in_, o, deps=(), free=False):
+        op("v", lambda: V.tensor_reduce(out, in_, X, o), deps, free)
+
+    def scan(out, d0, d1, init, o0, o1, deps=(), free=False):
+        op("v", lambda: V.tensor_tensor_scan(out, d0, d1, init, o0, o1), deps, free)
+
+    def mset(ap, c, deps=(), free=True):
+        op("v", lambda: V.memset(ap, c), deps, free)
+
+    def quant(name, a, b, src, deps=(), free=False):
+        op("v", lambda: V.quantize_mx(T[name + "q"][:, a:b], T[name + "s"][:, a:b], src), deps, free)
+
+    def act(out, in_, deps=(), free=False):
+        op("s", lambda: S.activation(out, in_, F.Copy), deps, free)
+
+    def mm(out, w, a, x, start, stop, deps, free=False):
+        op("p", lambda: P.matmul_mx(out, T[w + "q"][:, a:a + 128], T[w + "s"][:, a:a + 128], T[x + "q"][:, 0:M], T[x + "s"][:, 0:M],
+                                    start, stop), deps, free)
+
+    def iota(out, pat, base, cm, flt=True):
+        if flt:
+            op("c", lambda: g.iota(out, pat, base, cm, allow_small_or_imprecise_dtypes=True), free=True)
+        else:
+            op("c", lambda: g.iota(out, pat, base, cm), free=True)
+
+    def pick(dst, d0, src, s1, off, n, deps=()):
+        dv = list(deps) + [tok("v")]
+        op("s", lambda: S.activation(T[dst + "s"][:, d0:d0 + n], T[src + "s"][:, 0:s1].indirect(off), F.Copy), dv)
+        cp(T[dst + "q"][:, d0:d0 + n].bitcast(dt.uint32), T[src + "q"][:, 0:s1].bitcast(dt.uint32).indirect(off), deps)
+        return [tok("v"), tok("s")]
+
+    pos = {"sm": 0, "ou": 0}
+
+    def take(b, n):
+        a = pos[b]
+        pos[b] = a + (n + 7) // 8 * 8
+        return a
+
+    def sm(n):
+        return take("sm", n)
+
+    SM, OU, IOT, NI = T.sm, T.ou, T.iot, T.ni
+
+    def u_(a, n):
+        return OU[:, a:a + n]
+
+    def ou(n):
+        return u_(take("ou", n), n)
+
+    def s_(a, n):
+        return SM[:, a:a + n]
+
+    peer = [q for q in near if q != r and cores[q] in topo.cores_of(core)]
+    offc = [q for q in near if q != r and q not in peer]
+    e_off = topo.engines(core, cores[offc[0]])
+    e_on = [e for e in topo.engines(core, cores[peer[0]]) if e not in e_off]
+    n_far = len(far) * (len(topo.engines(hands[0][0], cores[far[0]])) // len(hands[0][1]))
+    sent = [0]
+
+    def send(items, deps):
+        for d in deps:
+            wait("c", d)
+        g.remote_dma_fused([RemoteDMATransfer(dst_ids=[_dst(topo, c, core)], dma_engine_mask=_mask(e), remote_sem=T.sem[s], src=a, dst=b)
+                            for c, e, s, a, b in items], local_sem=T.sem.ls)
+        sent[0] += sum(len(it[1]) for it in items)
+
+    def spread(src, dst, sem, hdst, hsem, deps, near_first=False):
+        if near_first:
+            eng = [e_off[0:4], e_off[4:8], e_on[0:4], e_on[4:6], e_on[6:8]]
+        else:
+            eng = [e_off[0:2], e_off[2:4], e_off[4:6], e_on[0:4], e_on[4:8]]
+        direct = [(cores[q], eng[k], sem, src, dst) for k, q in enumerate(offc + peer)]
+        handed = [(hands[k][0], eng[3 + k], hsem, src, hdst) for k in range(2)]
+        send(direct + handed if near_first else handed + direct, deps)
+        return 12 if near_first else 6
+
+    def arrival(sem, n):
+        total[sem] = n
+        return (sem, n)
+
+    t_x = dma("y", T.xt[:], T.x[:], "dx")
+    t_u = dma("s", T.ut[:], T.u[:], "du")
+    half = 64 * (qa // 2)
+    for k in range(4):
+        t_n = dma("y" if k % 2 == 0 else "s", T.nbw[half + 16 * k:half + 16 * k + 16, :], T.nb[:], "dn")
+    t_w = dma("y", T.wt[:], T.w[:], "dw")
+
+    iota(T.pi[:, 0:1], [[0, 1]], 0, 1, flt=False)
+    iota(IOT[:, 0:256], [[1, 256]], 0, 0)
+    iota(T.j16[:, 0:96], [[0, 6], [1, 16]], 0, 0)
+    t_p = tok("c")
+    iota(T.ci[:, 0:96], [[1, 48], [0, 2]], 0, 0, flt=False)
+    iota(T.ci[:, 96:104], [[16, 4], [0, 2]], 0, 0, flt=False)
+    iota(T.fw[:, 0:48], [[0, 4], [1, 12]], 0, 0)
+    t_c1 = tok("c")
+    for k in range(1, 6):
+        op("s", lambda: S.activation(IOT[:, 256 * k:256 * k + 256], IOT[:, 0:256], F.Identity, bias=float(256 * k)), [t_p], free=True)
+
+    mset(T.nbw[64 - half:128 - half, :], 0)
+    mset(SM[:], 0.0)
+    o_ut = [ou(8) for _ in range(R)]
+    for t in range(R):
+        mset(o_ut[t], t)
+    PI, PF = T.pi, T.pf
+    ts(PI[:, 1:2], PI[:, 0:1], 15, A.bitwise_and, deps=[t_p], free=True)
+    ts(PI[:, 2:3], PI[:, 0:1], 4, A.logical_shift_right, 1, A.bitwise_and, free=True)
+    ts(PI[:, 3:4], PI[:, 0:1], 5, A.logical_shift_right, free=True)
+    ts(PI[:, 4:5], PI[:, 0:1], 1, A.bitwise_and, free=True)
+    ts(PI[:, 5:6], PI[:, 0:1], 31, A.bitwise_and, free=True)
+    cp(PF[:, 0:6], PI[:, 0:6])
+    pP, pI, pS, pA, pO, pR = [PF[:, k:k + 1] for k in range(6)]
+    c0 = sm(16)
+    col = [s_(c0 + k, 1) for k in range(16)]
+    tt(col[0], pI, pS, A.add)
+    ts(col[1], pA, float(qa), A.not_equal, 20.0, A.mult, free=True)
+    ts(col[0], col[0], 2.0, A.mult, pO, A.subtract)
+    o_nb = ou(1)
+    ts(o_nb, col[0], col[1], A.add, 35.0, A.min)
+    cp(T.nbs[:], T.nbw[:, 0:36].indirect(o_nb), deps=[t_n])
+    t_nbs = tok("v")
+    nd = spread(T.nbs[:, 0:10], T.nbl[:, 10 * r:10 * r + 10], "an", T.rn[:, 0:10], "rn", [t_nbs])
+    t_an = [arrival("an", nd + n_far), dma("y", T.nbl[:, 10 * r:10 * r + 10], T.nbs[:, 0:10], "on", [t_nbs])]
+
+    quant("u", 0, 128, T.ut[:], [t_u])
+    t_ur = pick("ur", 0, "u", 128, o_ut[0], 128)
+    quant("on0", 0, M, T.xt[:], [t_x], free=True)
+    t_state = [tok("v")]
+
+    def heights(t, deps):
+        mm(T.ph[:, 0:M], "ur", 128 * t, "on%d" % t, True, True, deps)
+        tr(T.ht[:], T.ph[:, 0:M], deps=[tok("p")])
+        HS = T.hs[:, 6 * t:6 * t + 6]
+        cp(HS, T.ht[:, 0:M:32])
+        tk = tok("v")
+        a = 64 * t + 6 * r
+        nd = spread(HS, T.hl[:, a:a + 6], "ah%d" % t, T.rh[:, 6 * t:6 * t + 6], "rh%d" % t, [tk])
+        return [arrival("ah%d" % t, nd + n_far), dma("y", T.hl[:, a:a + 6], HS, "oh%d" % t, [tk])]
+
+    for k in range(1, 6):
+        act(T.j16[:, 96 * k:96 * k + 96], T.j16[:, 0:96], free=True)
+    t_iot = tok("s")
+    t_h = heights(0, t_state + t_ur)
+
+    iota(T.fw[:, 48:84], [[6, 3], [10, 2], [1, 6]], 0, 0)
+    iota(T.fw2[:, 0:36], [[6, 3], [0, 2], [1, 6]], 0, 0)
+    iota(T.fw[:, 96:112], [[64, 8], [16, 2]], 0, 0)
+    iota(T.fw[:, 144:192], [[1, 8], [0, 6]], 40, 0)
+    iota(T.fw[:, 192:240], [[1, 8], [0, 6]], 41, 0)
+    iota(T.fw[:, 288:320], [[1, 16], [32, 2]], 0, 0)
+    t_c2 = tok("c")
+    for out, n in ((T.cw[:, 0:848], 848), (T.cw[:, 848:1696], 848), (T.et[:, 0:1024], 1024), (T.et[:, 1024:2048], 1024)):
+        op("s", lambda: S.activation(out, IOT[:, 0:n], F.Copy, scale=0.0))
+    t_zero = tok("s")
+    for t in range(R):
+        mset(T.hl[:, 64 * t + 48:64 * t + 64], 0.0)
+    ts(T.diag[:], T.j16[:, 0:320], pI, A.is_equal, deps=[t_c1, t_iot], free=True)
+    ts(T.rs16[:], T.j16[:], 0.0, A.is_gt, free=True)
+    mset(T.fw[:, 84:96], 0.0)
+    mset(T.fw[:, 112:128], 0.0)
+    mset(T.fw[:, 136:144], 0.0)
+    order = near + far
+    for q in range(N):
+        mset(T.fw[:, 240 + 6 * q:246 + 6 * q], float(near.index(q) if q in near else 32 + far.index(q)))
+        mset(T.fw[:, 128 + q:129 + q], float(order.index(q)))
+    o_b, o_own = ou(1), ou(1)
+    u0_, e0 = take("ou", 8), take("ou", 96)
+    o_dup = u_(u0_, 8)
+    k_i, k_n, n_f, n_w, n_id, ones, stp = sm(3), sm(3), sm(6), sm(12), sm(48), sm(32), sm(3)
+    ts(col[2], pS, 32.0, A.mult, free=True)
+    ts(col[3], pA, 12.0, A.mult, free=True)
+    spot = [K if j == jo else 12 * j for j in range(4)]
+    ts(col[4], pI, 11.0, A.min, float(spot[0]), A.add, free=True)
+    ts(col[5], pI, 11.0, A.min, float(12 * jo), A.add, free=True)
+    ts(col[6], pR, 2.0, A.add, free=True)
+    ts(col[12], pR, 2.5, A.add, -1.0, A.mult, free=True)
+    ts(col[7], pA, 384.0, A.mult, pR, A.add, free=True)
+    cp(u_(e0, 96), T.ci[:, 0:96], free=True)
+    ts(o_dup, T.ci[:, 96:104], pI, A.add, free=True)
+    ts(s_(k_i, 3), IOT[:, 0:48:16], pI, A.add, free=True)
+    ts(s_(n_f, 6), IOT[:, 0:192:32], pR, A.add, 1.0 / 1024, A.mult, free=True)
+    ts(s_(n_w, 12), IOT[:, 0:192:16], pI, A.add, free=True)
+    mset(s_(ones, 32), 1.0)
+    mset(T.rs32[:], 1.0)
+    for j in range(3):
+        mset(s_(stp + j, 1), float(spot[j + 1] - spot[j]))
+    ts(T.fw2[:, 0:36], T.fw2[:, 0:36], 10.0, A.is_ge, 10.0, A.mult, deps=[t_c2], free=True)
+    tt(T.fw[:, 48:84], T.fw[:, 48:84], T.fw2[:, 0:36], A.add)
+    ts(o_own, pI, 11.0, A.min, col[3], A.add, free=True)
+    ts(s_(k_n, 3), s_(k_i, 3), 1.0, A.add, -1.0, A.mult, free=True)
+    mset(T.rs32[:, 0:192:32], 0.0)
+    ts(s_(n_id + 36, 12), IOT[:, 0:384:32], col[7], A.add, free=True)
+    tt(T.fw2[:], T.fw[:], T.diag[:], A.mult)
+    scan(T.fw[:], T.rs16[:, 0:320], T.fw2[:], 0.0, A.mult, A.add)
+    o_m, o_nbf, o_eg, o_lo, o_hi, o_of, o_il = ou(3), ou(3), ou(1), ou(3), ou(3), ou(3), ou(2)
+    force["v"] = True
+    for dst, a, n in ((o_m, 0, 3), (o_nbf, 3, 3), (o_eg, 8, 1), (o_lo, 9, 3), (o_hi, 12, 3), (o_of, 15, 3), (o_il, 18, 2)):
+        cp(dst, T.fw[:, 16 * a + 15:16 * (a + n):16], free=True)
+    ts(o_b, T.fw[:, 111:112], col[2], A.add, 383.0, A.min, free=True)
+
+    nbx = sm(40)
+    for a in range(4):
+        for part in range(2):
+            s0 = 32 * (a ^ part)
+            cp(SM[32 * a:32 * a + 32, nbx + 20 * part:nbx + 20 * part + 20], T.nbl[s0:s0 + 32, 20 * a:20 * a + 20], deps=t_an, free=True)
+    cp(NI[:, 0:48], s_(nbx, 40).indirect(o_nbf))
+    ts(NI[:, 192:228], NI[:, 0:36], 15, A.bitwise_and)
+    ts(NI[:, 48:84], NI[:, 0:36], 10, A.logical_shift_right, free=True)
+    ts(NI[:, 96:132], NI[:, 0:36], 4, A.logical_shift_right, 1, A.bitwise_and, free=True)
+    ts(NI[:, 144:180], NI[:, 0:36], 5, A.logical_shift_right, 31, A.bitwise_and, free=True)
+    o_nh, o_nl, o_nn = ou(36), ou(36), ou(36)
+    cp(o_nn, NI[:, 0:36], free=True)
+    cp(o_nl, NI[:, 192:228])
+    ts(NI[:, 48:84], NI[:, 48:84], 64.0, A.mult, free=True)
+    ts(NI[:, 96:132], NI[:, 96:132], 32.0, A.mult, free=True)
+    act(T.mk[:], T.diag[:, 0:16].indirect(o_nl), deps=[tok("v")])
+    t_mk = tok("s")
+    act(T.g3t[:], IOT[:].indirect(o_nn))
+    t_id = tok("s")
+    tt(NI[:, 48:84], NI[:, 48:84], NI[:, 96:132], A.add)
+    tt(NI[:, 48:84], NI[:, 48:84], NI[:, 144:180], A.add)
+    cp(o_nh, NI[:, 48:84])
+    x0 = 160 + M * r
+    cp(T.cw[:, x0:x0 + 16], T.diag[:, 0:16], deps=[t_zero], free=True)
+    ts(T.cw[:, x0 + 16:x0 + 32], T.diag[:, 0:16], 4096.0, A.mult, free=True)
+
+    z64, y128, t16, m24, m12, e48, f24, f12 = sm(64), sm(128), sm(128), sm(24), sm(16), sm(48), sm(24), sm(32)
+    kk, ka, kb, wa, cc = sm(8), sm(8), sm(32), sm(32), sm(64)
+    kt, kd, szw, fcol, enc, lmin = z64, z64 + 32, y128, m12, f12, f24
+    wt_, wx, pre, aa, ab, ef, eg = y128 + 32, y128 + 64, m24, m24 + 8, m24 + 9, f24, e48
+    o_l, o_p0, o_p1, o_p2, o_c, o_s = ou(3), ou(1), ou(3), ou(1), ou(12), ou(12)
+    a0, r0, d0, f0, b0 = take("ou", 12), take("ou", 12), take("ou", 32), take("ou", 96), take("ou", 16)
+    o_a, o_r = u_(a0, 12), u_(r0, 12)
+    H = M // 2
+    src = [T.g1t, H]
+
+    def hop(tab, deps, conv=True):
+        if conv:
+            cp(u_(a0, 6), T.g1t[:, 0:H:16], q="x")
+            cp(u_(a0 + 6, 6), src[0][:, src[1]:src[1] + H:16], q="z")
+        act(T.gy[:], tab[:].indirect(u_(a0 + 6, 6)), deps=[tok("z")] + deps)
+        cp(T.g1[:, 0:H], tab[:].indirect(u_(a0, 6)), deps, q="x")
+        tr(T.g1t[:, 0:H], T.g1[:, 0:H], q="x")
+        tr(T.gyt[:], T.gy[:], [tok("s")], q="z")
+        src[0:2] = [T.gyt, 0]
+
+    def doubled(tab, deps):
+        cp(u_(d0, 12), T.g1t[:, 0:H:8], q="x")
+        cp(u_(d0 + 12, 12), src[0][:, src[1]:src[1] + H:8], q="z")
+        act(T.g2[:, 192:384], tab[:].indirect(u_(d0 + 12, 12)), deps=[tok("z")] + deps)
+        cp(T.g2[:, 0:192], tab[:].indirect(u_(d0, 12)), deps, q="x")
+        tr(T.g2t[:, 0:192], T.g2[:, 0:192], q="x")
+        tr(T.g2t[:, 192:384], T.g2[:, 192:384], [tok("s")], q="z")
+
+    def rebuild(tab, new, first):
+        both = [tok("x"), tok("z"), tok("v")]
+
+        def rep(a, d, q):
+            s = OU[32 * a:32 * a + 32, d0:d0 + 24] if first else T.g2t[32 * a:32 * a + 32, 0:384:16]
+            cp(OU[32 * d:32 * d + 32, f0 + 24 * a:f0 + 24 * a + 24], s, both, free=True, q=q)
+        for a, d in ((0, 0), (0, 1), (1, 1), (1, 0)):
+            rep(a, d, "x")
+        rep(2, 2, "z")
+        cp(OU[64:128, f0:f0 + 48], OU[0:64, f0:f0 + 48], q="x")
+        act(new[:, 0:768], tab[:].indirect(u_(f0, 48)), deps=[tok("x")])
+        for a, d in ((2, 3), (3, 3), (3, 2)):
+            rep(a, d, "z")
+        if not first:
+            cp(u_(b0, 16), T.g2t[:].indirect(o_b), q="x")
+        cp(OU[0:64, f0 + 48:f0 + 96], OU[64:128, f0 + 48:f0 + 96], q="z")
+        ns = FIRST_S if first else WIDE_S
+        act(new[:, 768:16 * ns], tab[:].indirect(u_(f0 + 48, ns - 48)), deps=[tok("z")], free=True)
+        if not first:
+            cp(T.g1[:], tab[:].indirect(u_(b0, 12)), q="x")
+        cp(new[:, 16 * ns:NN], tab[:].indirect(u_(f0 + ns, 96 - ns)), q="z")
+        if not first:
+            tr(T.g1t[:], T.g1[:], q="x")
+            src[0:2] = [T.g1t, H]
+            wait("z", tok("x"))
+        return [tok("s"), tok("z")]
+
+    def cumul(dst):
+        tr(s_(wt_, 32), s_(wa, 32))
+        red(col[8], s_(wt_, 32), A.add)
+        ts(s_(wx, 32), s_(ones, 32), col[8], A.mult)
+        tr(s_(dst, 32), s_(wx, 32))
+
+    for t in range(R):
+        on, nx = "on%d" % t, "on%d" % (t + 1)
+        act(T.sc[:, 591:832:16], T.hl[:, 64 * t:64 * t + 48].indirect(o_own), deps=t_h + [tok("v")])
+        t_oh = tok("s")
+        tr(s_(z64, 64), T.hl[:, 64 * t:64 * t + 64], deps=t_h)
+        cp(s_(y128, 128), s_(z64, 64).indirect(o_dup))
+        tr(s_(t16, 128), s_(y128, 128))
+        tt(T.g3[:], s_(t16, 128).indirect(o_nh), T.mk[:], A.mult, deps=[t_mk])
+        if t == 0:
+            tr(T.sc[:, 0:576], T.g3t[:], deps=[t_id], free=True)
+            cp(s_(n_id, 36), T.sc[:, 0:576:16])
+            ts(s_(n_id, 48), s_(n_id, 48), -1.0, A.mult, 4096.0, A.add)
+        tr(T.g3t[:], T.g3[:])
+        scan(T.sc[:, 0:576], T.rs16[:], T.g3t[:], 0.0, A.mult, A.add)
+        tt(s_(m24, 24), T.sc[:, 15:384:16], T.sc[:, 399:768:16], A.max, deps=[t_oh])
+        tt(s_(m12, 12), s_(m24, 12), s_(m24 + 12, 12), A.max)
+        tt(s_(e48, 48), s_(m12, 12).indirect(o_m), T.sc[:, 15:768:16], A.is_equal)
+        tt(s_(e48, 48), s_(e48, 48), s_(n_id, 48), A.mult)
+        tt(s_(f24, 24), s_(e48, 24), s_(e48 + 24, 24), A.max)
+        tt(s_(f12, 12), s_(f24, 12), s_(f24 + 12, 12), A.max)
+        tr(s_(z64, 32), s_(f12, 32))
+        ts(o_a, s_(f12, 12), -1.0, A.mult, 4096.0, A.add, free=True)
+        cp(s_(y128, 64), s_(z64, 32).indirect(u_(u0_, 4)))
+        tr(s_(t16, 64), s_(y128, 64))
+        ts(u_(d0, 32), s_(t16, 64).indirect(o_il), -1.0, A.mult, 4096.0, A.add)
+        tab, oth = T.ta, T.tb
+        dep = rebuild(IOT, tab, True)
+        for lv, k in enumerate(LEVELS):
+            for h in range(k):
+                hop(tab, dep, bool(lv or h))
+            doubled(tab, dep)
+            dep = rebuild(tab, oth, False)
+            tab, oth = oth, tab
+        for h in range(TAIL):
+            hop(tab, dep)
+        cp(u_(a0, 6), T.g1t[:, 0:H:16], [tok("x")])
+        cp(u_(a0 + 6, 6), T.gyt[:, 0:H:16], [tok("z")], free=True)
+        tk = tok("v")
+        for k in range(4):
+            op("s", lambda: S.activation(T.sj[:, 0:M] if k % 2 else T.sj[:, M:2 * M], T.cw[:, 160 - 32 * k:160 - 32 * k + NN].indirect(o_a), F.Copy,
+                                         accum_out=s_(kk + k, 1)), [tk], free=(k % 2 == 1))
+        cp(T.w1[:], T.cw[:, 32:32 + NN].indirect(o_a))
+        cp(T.w2[:], T.cw[:, 0:NN].indirect(o_a), free=True)
+        red(s_(kk + 4, 1), T.w1[:], A.add)
+        red(s_(kk + 5, 1), T.w2[:], A.add, free=True)
+        tt(SM[0:64, ka:ka + 6], SM[0:64, kk:kk + 6], SM[64:128, kk:kk + 6], A.add, deps=[tok("s")])
+        tt(SM[0:32, kb:kb + 6], SM[0:32, ka:ka + 6], SM[32:64, ka:ka + 6], A.add)
+        tr(SM[0:32, kt:kt + 32], SM[0:32, kb:kb + 32])
+        tt(NI[0:32, 0:16], SM[0:32, kt:kt + 16], SM[0:32, kt + 16:kt + 32], A.add)
+        ts(NI[0:32, 16:32], NI[0:32, 0:16], 4095, A.bitwise_and)
+        ts(NI[0:32, 32:48], NI[0:32, 0:16], 12, A.logical_shift_right, free=True)
+        ts(SM[0:32, kd:kd + 32], NI[0:32, 16:48], 33.0, A.min)
+        tr(SM[0:32, szw:szw + 32], SM[0:32, kd:kd + 32])
+        force["v"] = True
+        for d in range(1, 4):
+            cp(SM[32 * d:32 * d + 32, szw:szw + 6], SM[0:32, szw:szw + 6], free=True)
+        cp(T.b1[:], s_(szw, 6).indirect(u_(e0, 12)))
+        tr(T.b2[:], T.b1[:])
+        op("s", lambda: S.activation(T.sj[:, 0:M], T.b2[:], F.Sign, bias=col[12], accum_out=col[11]), [tok("v")])
+        ts(T.b3[:], T.b2[:], col[6], A.is_equal)
+        red(s_(fcol + 1, 1), T.b3[:], A.add)
+        MS = T.ms[:, 2 * t:2 * t + 2]
+        cp(T.ms[:, 2 * t:2 * t + 1], s_(fcol + 1, 1))
+        ts(T.ms[:, 2 * t + 1:2 * t + 2], col[11], -0.5, A.mult, float(K // len(near) - M // 2), A.add, deps=[tok("s")], free=True)
+        a = 32 * t + 8 * jo
+        nd = spread(MS, T.lea[:, a:a + 2], "aa%d" % t, T.rm[:, 2 * t:2 * t + 2], "rm%d" % t, [tok("v")], near_first=True)
+        t_aa, t_ab = [arrival("aa%d" % t, nd)], [arrival("ab%d" % t, n_far)]
+        ts(s_(fcol, 1), col[11], 0.5, A.mult, float(M // 2), A.add)
+        cp(T.lea[:, a:a + 2], MS, free=True)
+        scan(T.b2[:], T.b3[:], T.b3[:], s_(fcol, 1), A.add, A.max)
+        tt(T.b1[:], T.b2[:], T.b3[:], A.mult)
+        tr(T.b2[:], T.b1[:])
+        scan(T.b1[:], T.rs32[:], T.b2[:], 0.0, A.mult, A.add)
+        tt(s_(enc, 6), T.b1[:, 31:M:32], s_(n_f, 6), A.add)
+        LW = T.lw[:, 6 * t:6 * t + 6]
+        cp(LW, T.b1[:, 31:M:32], free=True)
+        tk = tok("v")
+        a = 48 * t + 6 * r
+        nd = spread(LW, T.lml[:, a:a + 6], "al%d" % t, T.rl[:, 6 * t:6 * t + 6], "rl%d" % t, [tk])
+        t_al = [arrival("al%d" % t, nd + n_far), dma("y", T.lml[:, a:a + 6], LW, "ol%d" % t, [tk])]
+        cp(T.w2[:], s_(enc, 6).indirect(u_(e0, 12)))
+        tr(T.w1[:], T.w2[:])
+        tk = tok("v")
+        tks = []
+        for c in range(2):
+            op("s", lambda: S.activation(T.sj[:, M * c:M * c + M], T.w1[:], F.Abs, bias=s_(k_n + c, 1)), [tk])
+            tks.append(tok("s"))
+        ts(T.w2[:], T.w1[:], s_(k_n + 2, 1), A.add)
+        op("v", lambda: V.tensor_reduce(s_(lmin + 2, 1), T.w2[:], X, A.min, apply_absolute_value=True))
+        for c in range(2):
+            red(s_(lmin + c, 1), T.sj[:, M * c:M * c + M], A.min, deps=[tks[c]], free=True)
+        ts(o_l, s_(lmin, 3), 1024.0, A.mult, float(M - 1), A.min)
+        qn, pa, la, pb, lb, rb, rc = ["%s%d" % (n, t) for n in ("qa", "pa", "la", "pb", "lb", "rb", "rc")]
+        t_qa = pick(qn, 0, on, M, o_l, K)
+        EA, EB = T.lea[:, 32 * t:32 * t + 32:8], T.leb[:, 8 * t:8 * t + 8:2]
+        scan(s_(pre, 4), EA, EA, 0.0, A.add, A.max, deps=t_aa)
+        red(s_(aa, 1), T.lea[:, 32 * t + 1:32 * t + 32:8], A.add, free=True)
+        ts(s_(wa + 1, 4), s_(pre, 4), s_(aa, 1), A.min, 0.0, A.max)
+        cumul(cc)
+        ts(o_p1, s_(k_i, 3), s_(cc + jo, 1), A.subtract, 0.0, A.max)
+        tk = pick(pa, 0, qn, K, o_p1, K, t_qa)
+        eng = {offc[0]: e_off[0:4], offc[1]: e_off[4:8], peer[0]: e_on[0:4]}
+        others = [(q, 12 * near.index(q)) for q in offc + peer]
+        send([(cores[q], eng[q], "a1%d" % t, _q(T, pa, a, a + 12), _q(T, la, 12 * jo, 12 * jo + 12)) for q, a in others], tk[0:1])
+        send([(cores[q], eng[q], "a1%d" % t, T[pa + "s"][:, a:a + 12], T[la + "s"][:, 12 * jo:12 * jo + 12]) for q, a in others], tk)
+        ts(o_p0, col[5], s_(cc + jo, 1), A.subtract, 0.0, A.max)
+        ts(s_(pre, 3), s_(cc + 1, 3), col[5], A.is_le, free=True)
+        t_a1 = [arrival("a1%d" % t, 24)] + pick(la, K, qn, K, o_p0, 16)
+        tt(s_(pre, 3), s_(pre, 3), s_(stp, 3), A.mult)
+        red(col[9], s_(pre, 3), A.add)
+        ts(o_p2, col[9], col[4], A.add)
+        doubled(IOT, [])
+        s0 = 192 * (r % 2)
+        for d in range(4):
+            cp(OU[32 * d:32 * d + 32, r0:r0 + 12], T.g2t[32 * qa:32 * qa + 32, s0:s0 + 192:16], [tok("x"), tok("z")], free=True)
+        RHO = T.rho[:, M * t:M * t + M]
+        act(RHO, IOT[:].indirect(o_r), deps=[tok("v")])
+        t_rho = tok("s")
+        dma("y", T.rt[0:1, M * t:M * t + M], T.rho[0:1, M * t:M * t + M], "out", [t_rho])
+        tk = pick(pb, 0, la, 64, o_p2, 16, t_a1)
+        a = 12 * jo
+        nd = spread(_q(T, pb, 0, 12), _q(T, lb, a, a + 12), "a2%d" % t, _q(T, rb, 0, 12), "r2%d" % t, tk[0:1])
+        spread(T[pb + "s"][:, 0:12], T[lb + "s"][:, a:a + 12], "a2%d" % t, T[rb + "s"][:, 0:12], "r3%d" % t, tk)
+        dma("y", _q(T, lb, a, a + 12), _q(T, pb, 0, 12), "o2%d" % t, tk)
+        t_a2 = [arrival("a2%d" % t, 2 * (nd + n_far)), dma("y", T[lb + "s"][:, a:a + 12], T[pb + "s"][:, 0:12], "o2%d" % t, tk)]
+        cp(s_(ef, 4), EA)
+        cp(s_(ef + 4, 4), EB, deps=t_ab, free=True)
+        scan(s_(pre, 4), EB, EB, 0.0, A.add, A.max, free=True)
+        red(s_(ab, 1), T.leb[:, 8 * t + 1:8 * t + 8:2], A.add, free=True)
+        cp(s_(eg, 16), s_(ef, 8).indirect(o_eg))
+        ts(s_(wa + 1, 4), s_(pre, 4), s_(ab, 1), A.min, 0.0, A.max, free=True)
+        ts(col[10], s_(aa, 1), s_(ab, 1), A.add, float(-K), A.add, free=True)
+        scan(s_(eg + 16, 8), s_(eg, 8), s_(eg, 8), 0.0, A.add, A.max)
+        ts(s_(wa + 9, 8), s_(eg + 16, 8), col[10], A.min, 0.0, A.max)
+        cumul(cc + 32)
+        ts(s_(cc + 32, 5), s_(cc + 32, 5), float(K), A.add)
+        tt(T.w3[:], RHO, IOT[:, M * r:M * r + M], A.not_equal, deps=[t_rho], free=True)
+        CC, LM = s_(cc, 64), T.lml[:, 48 * t:48 * t + 48]
+        u0, u1, u2, VAL = T.w1[:, 0:48], T.w1[:, 48:96], T.w1[:, 96:144], T.w2[:, 48:96]
+        cp(u0, CC.indirect(o_lo))
+        tt(u1, CC.indirect(o_of), LM, A.add, deps=t_al, free=True)
+        ts(u2, LM, 0.0, A.is_gt, free=True)
+        tt(T.w2[:, 0:48], CC.indirect(o_hi), u0, A.subtract)
+        tt(u1, u1, u2, A.mult, free=True)
+        tt(u0, LM, T.w2[:, 0:48], A.is_le)
+        tt(VAL, u0, u1, A.mult)
+        act(T.ex[:, 0:512], VAL.indirect(u_(e0, 32)), deps=[tok("v")])
+        tk1 = tok("s")
+        act(T.ex[:, 512:1024], VAL.indirect(u_(e0 + 32, 32)))
+        tk2 = tok("s")
+        cp(T.ex[:, 1024:NN], VAL.indirect(u_(e0 + 64, 32)))
+        tt(T.w4[:], T.w3[:], T.diag[:, 0:M], A.mult, free=True)
+        tr(T.vw[:, 1024:NN], T.ex[:, 1024:NN])
+        tr(T.vw[:, 0:512], T.ex[:, 0:512], deps=[tk1], free=True)
+        tr(T.vw[:, 512:1024], T.ex[:, 512:1024], deps=[tk2], free=True)
+        tt(T.w1[:], T.vw[:].indirect(o_r), T.w4[:], A.mult)
+        scan(T.w3[:], T.rs16[:, 0:M], T.w1[:], 0.0, A.mult, A.add)
+        ts(o_c, T.w3[:, 15:M:16], -1.0, A.add, 0.0, A.max)
+        ts(s_(f12, 12), T.w3[:, 15:M:16], 0.0, A.is_gt, float(M), A.mult, free=True)
+        tt(s_(f24, 12), s_(f12, 12), s_(n_w, 12), A.add)
+        cp(o_s, s_(f24, 12))
+        if t == 0:
+            for b in range(4):
+                ts(T.et[:, 512 * b + b:512 * b + 512:4], IOT[:, 0:128], pP, A.is_equal, free=True)
+            quant("e", 0, 512, T.et[:])
+            t_state = t_state + [tok("v")]
+        for b in range(4):
+            mm(T.pd[:, 512 * b:512 * b + M], "e", 128 * b, on, True, False, t_state, free=True)
+        if t + 1 < R:
+            pick("ur", 128 * (t + 1), "u", 128, o_ut[t + 1], 128)
+        else:
+            quant("w", 0, 128, T.wt[:], [t_w])
+        tk = pick(rc, 0, lb, 2 * K, o_c, M, t_a2)
+        tb = []
+        for b in range(4):
+            mm(T.pd[:, 512 * b:512 * b + M], "e", 128 * b, rc, False, True, tk, free=(b % 2 == 1))
+            if b % 2 == 1:
+                tb.append(tok("p"))
+        for b in (0, 2):
+            op("s", lambda: S.activation(T.nt[:, b:4 * M:4], T.pd[:, 512 * b:512 * b + M], F.Copy, scale=0.5), [tb[b // 2]], free=True)
+            ts(T.nt[:, b + 1:4 * M:4], T.pd[:, 512 * b + 512:512 * b + 512 + M], 0.5, A.mult, deps=[tb[b // 2]], free=True)
+        quant(on, M, 2 * M, T.nt[:], [tok("s")])
+        t_state = pick(nx, 0, on, 2 * M, o_s, M)
+        if t + 1 < R:
+            t_h = heights(t + 1, t_state)
+
+    on = "on%d" % R
+    mm(T.ph[:, 0:M], "w", 0, on, True, True, t_state)
+    dma("y", T.oc[:, 0:4 * M], _q(T, on, 0, M), "out", t_state)
+    for k in range(4):
+        dma("s", T.osc[4 * k:4 * k + 4, 0:M], T[on + "s"][32 * k:32 * k + 4, 0:M], "out", t_state)
+    cp(T.yb[:], T.ph[:, 0:M], deps=[tok("p")])
+    dma("y", T.y[:], T.yb[:], "out", [tok("v")])
+    for q in "vxzspc":
+        wait("c", (q, cnt[q]))
+    wait("c", ("ls", sent[0]))
+    for name in total:
+        wait("c", (name, total[name]))

@@ -3,20 +3,20 @@ from concourse.mybir import dt, AluOpType, AxisListType, ActivationFunctionType
 
 N, M, K, J, R = 8, 192, 48, 3, 3
 NN = N * M
-LEVELS = [2, 2, 2, 0]
-TAIL = 4
-FIRST_S = 52
-WIDE_S = 64
+WIDE0 = 2
+LEVELS = [(2, 2), (2, 2), (1, 1)]
+TAIL = 2
+FIRST_S = 54
 HAND_ENG = 4
 C4, U8, F32, B16, I32, U16 = "float8_e4m3fn_x4", "uint8", "float32", "bfloat16", "int32", "uint16"
 
 SCRATCH = {"pd": ("psum", [128, 2048], F32), "ph": ("psum", [128, 512], F32)}
 for _d, _l in (
-        (B16, (("xt", 768), ("ut", 512), ("wt", 512), ("et", 2048), ("nt", 768), ("ms", 2 * R), ("lea", 32 * R), ("leb", 8 * R),
+        (B16, (("xt", 768), ("ut", 512), ("wt", 512), ("et", 2048), ("nt", 768), ("ms", 200 * R), ("lea", 32 * R), ("leb", 8 * R),
                ("lw", 6 * R), ("lml", 48 * R), ("rm", 2 * R), ("rl", 6 * R), ("ex", NN), ("vw", NN), ("rs32", 192),
                ("b1", 192), ("b2", 192), ("b3", 192))),
         (F32, (("pf", 8), ("iot", NN), ("ta", NN), ("tb", NN), ("j16", 576), ("diag", 320), ("rs16", 576), ("fw", 320),
-               ("fw2", 320), ("cw", 1696), ("sm", 832), ("hs", 6 * R), ("hl", 64 * R), ("rh", 6 * R), ("mk", 576), ("g3", 576),
+               ("fw2", 320), ("cw", 1664), ("sm", 832), ("hs", 6 * R), ("hl", 64 * R), ("rh", 6 * R), ("mk", 576), ("g3", 576),
                ("g3t", 576), ("sc", 832), ("ht", 192), ("g2", 384), ("g2t", 384), ("w1", 192), ("w2", 192), ("w3", 192), ("w4", 192),
                ("sj", 384), ("rho", 192 * R), ("yb", 192), ("gy", 96), ("gyt", 96))),
         ("float16", (("g1", 192), ("g1t", 192))),
@@ -227,45 +227,45 @@ def rank_program(g, core, T, topo):
                             for c, e, s, a, b in items], local_sem=T.sem.ls)
         sent[0] += sum(len(it[1]) for it in items)
 
-    def spread(src, dst, sem, hdst, hsem, deps, near_first=False):
+    def spread(src, dst, sem, hdst, hsem, deps, near_first=False, apart=False):
         if near_first:
             eng = [e_off[0:4], e_off[4:8], e_on[0:4], e_on[4:6], e_on[6:8]]
         else:
             eng = [e_off[0:2], e_off[2:4], e_off[4:6], e_on[0:4], e_on[4:8]]
         direct = [(cores[q], eng[k], sem, src, dst) for k, q in enumerate(offc + peer)]
         handed = [(hands[k][0], eng[3 + k], hsem, src, hdst) for k in range(2)]
-        send(direct + handed if near_first else handed + direct, deps)
+        if apart:
+            send(handed, deps)
+            send(direct, deps)
+        else:
+            send(direct + handed if near_first else handed + direct, deps)
         return 12 if near_first else 6
 
     def arrival(sem, n):
         total[sem] = n
         return (sem, n)
 
-    t_x = dma("y", T.xt[:], T.x[:], "dx")
-    t_u = dma("s", T.ut[:], T.u[:], "du")
     half = 64 * (qa // 2)
     for k in range(4):
         t_n = dma("y" if k % 2 == 0 else "s", T.nbw[half + 16 * k:half + 16 * k + 16, :], T.nb[:], "dn")
+    t_x = dma("y", T.xt[:], T.x[:], "dx")
+    t_u = dma("s", T.ut[:], T.u[:], "du")
     t_w = dma("y", T.wt[:], T.w[:], "dw")
 
     iota(T.pi[:, 0:1], [[0, 1]], 0, 1, flt=False)
+    t_p0 = tok("c")
     iota(IOT[:, 0:256], [[1, 256]], 0, 0)
     iota(T.j16[:, 0:96], [[0, 6], [1, 16]], 0, 0)
     t_p = tok("c")
     iota(T.ci[:, 0:96], [[1, 48], [0, 2]], 0, 0, flt=False)
     iota(T.ci[:, 96:104], [[16, 4], [0, 2]], 0, 0, flt=False)
-    iota(T.fw[:, 0:48], [[0, 4], [1, 12]], 0, 0)
     t_c1 = tok("c")
     for k in range(1, 6):
         op("s", lambda: S.activation(IOT[:, 256 * k:256 * k + 256], IOT[:, 0:256], F.Identity, bias=float(256 * k)), [t_p], free=True)
 
     mset(T.nbw[64 - half:128 - half, :], 0)
-    mset(SM[:], 0.0)
-    o_ut = [ou(8) for _ in range(R)]
-    for t in range(R):
-        mset(o_ut[t], t)
     PI, PF = T.pi, T.pf
-    ts(PI[:, 1:2], PI[:, 0:1], 15, A.bitwise_and, deps=[t_p], free=True)
+    ts(PI[:, 1:2], PI[:, 0:1], 15, A.bitwise_and, deps=[t_p0], free=True)
     ts(PI[:, 2:3], PI[:, 0:1], 4, A.logical_shift_right, 1, A.bitwise_and, free=True)
     ts(PI[:, 3:4], PI[:, 0:1], 5, A.logical_shift_right, free=True)
     ts(PI[:, 4:5], PI[:, 0:1], 1, A.bitwise_and, free=True)
@@ -279,9 +279,12 @@ def rank_program(g, core, T, topo):
     ts(col[0], col[0], 2.0, A.mult, pO, A.subtract)
     o_nb = ou(1)
     ts(o_nb, col[0], col[1], A.add, 35.0, A.min)
+    o_ut = [ou(8) for _ in range(R)]
+    for t in range(R):
+        mset(o_ut[t], t)
     cp(T.nbs[:], T.nbw[:, 0:36].indirect(o_nb), deps=[t_n])
     t_nbs = tok("v")
-    nd = spread(T.nbs[:, 0:10], T.nbl[:, 10 * r:10 * r + 10], "an", T.rn[:, 0:10], "rn", [t_nbs])
+    nd = spread(T.nbs[:, 0:10], T.nbl[:, 10 * r:10 * r + 10], "an", T.rn[:, 0:10], "rn", [t_nbs], apart=True)
     t_an = [arrival("an", nd + n_far), dma("y", T.nbl[:, 10 * r:10 * r + 10], T.nbs[:, 0:10], "on", [t_nbs])]
 
     quant("u", 0, 128, T.ut[:], [t_u])
@@ -304,6 +307,7 @@ def rank_program(g, core, T, topo):
     t_iot = tok("s")
     t_h = heights(0, t_state + t_ur)
 
+    iota(T.fw[:, 0:48], [[0, 4], [1, 12]], 0, 0)
     iota(T.fw[:, 48:84], [[6, 3], [10, 2], [1, 6]], 0, 0)
     iota(T.fw2[:, 0:36], [[6, 3], [0, 2], [1, 6]], 0, 0)
     iota(T.fw[:, 96:112], [[64, 8], [16, 2]], 0, 0)
@@ -311,12 +315,13 @@ def rank_program(g, core, T, topo):
     iota(T.fw[:, 192:240], [[1, 8], [0, 6]], 41, 0)
     iota(T.fw[:, 288:320], [[1, 16], [32, 2]], 0, 0)
     t_c2 = tok("c")
-    for out, n in ((T.cw[:, 0:848], 848), (T.cw[:, 848:1696], 848), (T.et[:, 0:1024], 1024), (T.et[:, 1024:2048], 1024)):
+    for out, n in ((T.cw[:, 0:832], 832), (T.cw[:, 832:1664], 832), (T.et[:, 0:1024], 1024), (T.et[:, 1024:2048], 1024)):
         op("s", lambda: S.activation(out, IOT[:, 0:n], F.Copy, scale=0.0))
     t_zero = tok("s")
+    mset(SM[:, 16:832], 0.0)
     for t in range(R):
         mset(T.hl[:, 64 * t + 48:64 * t + 64], 0.0)
-    ts(T.diag[:], T.j16[:, 0:320], pI, A.is_equal, deps=[t_c1, t_iot], free=True)
+    ts(T.diag[:], T.j16[:, 0:320], pI, A.is_equal, deps=[t_c1, t_iot])
     ts(T.rs16[:], T.j16[:], 0.0, A.is_gt, free=True)
     mset(T.fw[:, 84:96], 0.0)
     mset(T.fw[:, 112:128], 0.0)
@@ -325,12 +330,14 @@ def rank_program(g, core, T, topo):
     for q in range(N):
         mset(T.fw[:, 240 + 6 * q:246 + 6 * q], float(near.index(q) if q in near else 32 + far.index(q)))
         mset(T.fw[:, 128 + q:129 + q], float(order.index(q)))
-    o_b, o_own = ou(1), ou(1)
+    o_b, o_b2, o_own = ou(1), ou(1), ou(1)
     u0_, e0 = take("ou", 8), take("ou", 96)
     o_dup = u_(u0_, 8)
-    k_i, k_n, n_f, n_w, n_id, ones, stp = sm(3), sm(3), sm(6), sm(12), sm(48), sm(32), sm(3)
+    k_i, k_n, n_f, n_w, n_id, ones, stp, zer = sm(3), sm(3), sm(6), sm(12), sm(48), sm(32), sm(3), sm(32)
     ts(col[2], pS, 32.0, A.mult, free=True)
     ts(col[3], pA, 12.0, A.mult, free=True)
+    ts(col[13], pI, 11.0, A.min, 32.0, A.mult, free=True)
+    ts(col[14], pS, 16.0, A.mult, free=True)
     spot = [K if j == jo else 12 * j for j in range(4)]
     ts(col[4], pI, 11.0, A.min, float(spot[0]), A.add, free=True)
     ts(col[5], pI, 11.0, A.min, float(12 * jo), A.add, free=True)
@@ -349,6 +356,7 @@ def rank_program(g, core, T, topo):
     ts(T.fw2[:, 0:36], T.fw2[:, 0:36], 10.0, A.is_ge, 10.0, A.mult, deps=[t_c2], free=True)
     tt(T.fw[:, 48:84], T.fw[:, 48:84], T.fw2[:, 0:36], A.add)
     ts(o_own, pI, 11.0, A.min, col[3], A.add, free=True)
+    ts(o_b2, col[13], col[14], A.add, free=True)
     ts(s_(k_n, 3), s_(k_i, 3), 1.0, A.add, -1.0, A.mult, free=True)
     mset(T.rs32[:, 0:192:32], 0.0)
     ts(s_(n_id + 36, 12), IOT[:, 0:384:32], col[7], A.add, free=True)
@@ -359,6 +367,16 @@ def rank_program(g, core, T, topo):
     for dst, a, n in ((o_m, 0, 3), (o_nbf, 3, 3), (o_eg, 8, 1), (o_lo, 9, 3), (o_hi, 12, 3), (o_of, 15, 3), (o_il, 18, 2)):
         cp(dst, T.fw[:, 16 * a + 15:16 * (a + n):16], free=True)
     ts(o_b, T.fw[:, 111:112], col[2], A.add, 383.0, A.min, free=True)
+    x0 = 128 + M * r
+    ts(T.cw[:, x0:x0 + 32], IOT[:, 0:32], pR, A.is_equal, deps=[t_zero], free=True)
+    ts(T.cw[:, x0 + 32:x0 + 64], IOT[:, 0:32], pR, A.is_equal, 4096.0, A.mult, free=True)
+    for b in range(4):
+        ts(T.et[:, 512 * b + b:512 * b + 512:4], IOT[:, 0:128], pP, A.is_equal, free=True)
+    quant("e", 0, 512, T.et[:])
+    t_state = t_state + [tok("v")]
+    for t in range(1, R):
+        pick("ur", 128 * t, "u", 128, o_ut[t], 128)
+    quant("w", 0, 128, T.wt[:], [t_w])
 
     nbx = sm(40)
     for a in range(4):
@@ -366,56 +384,53 @@ def rank_program(g, core, T, topo):
             s0 = 32 * (a ^ part)
             cp(SM[32 * a:32 * a + 32, nbx + 20 * part:nbx + 20 * part + 20], T.nbl[s0:s0 + 32, 20 * a:20 * a + 20], deps=t_an, free=True)
     cp(NI[:, 0:48], s_(nbx, 40).indirect(o_nbf))
+    o_nh, o_nl, o_nn = ou(36), take("ou", 36), ou(36)
     ts(NI[:, 192:228], NI[:, 0:36], 15, A.bitwise_and)
-    ts(NI[:, 48:84], NI[:, 0:36], 10, A.logical_shift_right, free=True)
-    ts(NI[:, 96:132], NI[:, 0:36], 4, A.logical_shift_right, 1, A.bitwise_and, free=True)
-    ts(NI[:, 144:180], NI[:, 0:36], 5, A.logical_shift_right, 31, A.bitwise_and, free=True)
-    o_nh, o_nl, o_nn = ou(36), ou(36), ou(36)
     cp(o_nn, NI[:, 0:36], free=True)
-    cp(o_nl, NI[:, 192:228])
-    ts(NI[:, 48:84], NI[:, 48:84], 64.0, A.mult, free=True)
-    ts(NI[:, 96:132], NI[:, 96:132], 32.0, A.mult, free=True)
-    act(T.mk[:], T.diag[:, 0:16].indirect(o_nl), deps=[tok("v")])
+    cp(u_(o_nl, 36), NI[:, 192:228])
+    act(T.mk[:, 0:384], T.diag[:, 0:16].indirect(u_(o_nl, 24)), deps=[tok("v")])
     t_mk = tok("s")
     act(T.g3t[:], IOT[:].indirect(o_nn))
     t_id = tok("s")
+    ts(NI[:, 48:84], NI[:, 0:36], 10, A.logical_shift_right)
+    ts(NI[:, 96:132], NI[:, 0:36], 4, A.logical_shift_right, 1, A.bitwise_and, free=True)
+    ts(NI[:, 144:180], NI[:, 0:36], 5, A.logical_shift_right, 31, A.bitwise_and, free=True)
+    ts(NI[:, 48:84], NI[:, 48:84], 2.0, A.mult)
+    cp(T.mk[:, 384:576], T.diag[:, 0:16].indirect(u_(o_nl + 24, 12)), free=True)
     tt(NI[:, 48:84], NI[:, 48:84], NI[:, 96:132], A.add)
+    ts(NI[:, 48:84], NI[:, 48:84], 32.0, A.mult)
     tt(NI[:, 48:84], NI[:, 48:84], NI[:, 144:180], A.add)
     cp(o_nh, NI[:, 48:84])
-    x0 = 160 + M * r
-    cp(T.cw[:, x0:x0 + 16], T.diag[:, 0:16], deps=[t_zero], free=True)
-    ts(T.cw[:, x0 + 16:x0 + 32], T.diag[:, 0:16], 4096.0, A.mult, free=True)
 
     z64, y128, t16, m24, m12, e48, f24, f12 = sm(64), sm(128), sm(128), sm(24), sm(16), sm(48), sm(24), sm(32)
-    kk, ka, kb, wa, cc = sm(8), sm(8), sm(32), sm(32), sm(64)
-    kt, kd, szw, fcol, enc, lmin = z64, z64 + 32, y128, m12, f12, f24
+    kk, ka, wa, cc = sm(8), sm(8), sm(32), sm(64)
+    fcol, enc, lmin = m12, f12, f24
     wt_, wx, pre, aa, ab, ef, eg = y128 + 32, y128 + 64, m24, m24 + 8, m24 + 9, f24, e48
     o_l, o_p0, o_p1, o_p2, o_c, o_s = ou(3), ou(1), ou(3), ou(1), ou(12), ou(12)
-    a0, r0, d0, f0, b0 = take("ou", 12), take("ou", 12), take("ou", 32), take("ou", 96), take("ou", 16)
+    a0, r0, d0, f0 = take("ou", 16), take("ou", 12), take("ou", 32), take("ou", 96)
     o_a, o_r = u_(a0, 12), u_(r0, 12)
     H = M // 2
-    src = [T.g1t, H]
 
     def hop(tab, deps, conv=True):
         if conv:
             cp(u_(a0, 6), T.g1t[:, 0:H:16], q="x")
-            cp(u_(a0 + 6, 6), src[0][:, src[1]:src[1] + H:16], q="z")
+            cp(u_(a0 + 6, 6), T.gyt[:, 0:H:16], q="z")
         act(T.gy[:], tab[:].indirect(u_(a0 + 6, 6)), deps=[tok("z")] + deps)
         cp(T.g1[:, 0:H], tab[:].indirect(u_(a0, 6)), deps, q="x")
         tr(T.g1t[:, 0:H], T.g1[:, 0:H], q="x")
         tr(T.gyt[:], T.gy[:], [tok("s")], q="z")
-        src[0:2] = [T.gyt, 0]
 
     def doubled(tab, deps):
         cp(u_(d0, 12), T.g1t[:, 0:H:8], q="x")
-        cp(u_(d0 + 12, 12), src[0][:, src[1]:src[1] + H:8], q="z")
+        cp(u_(d0 + 12, 12), T.gyt[:, 0:H:8], q="z")
         act(T.g2[:, 192:384], tab[:].indirect(u_(d0 + 12, 12)), deps=[tok("z")] + deps)
         cp(T.g2[:, 0:192], tab[:].indirect(u_(d0, 12)), deps, q="x")
         tr(T.g2t[:, 0:192], T.g2[:, 0:192], q="x")
         tr(T.g2t[:, 192:384], T.g2[:, 192:384], [tok("s")], q="z")
 
-    def rebuild(tab, new, first):
+    def rebuild(tab, first, wides, hops):
         both = [tok("x"), tok("z"), tok("v")]
+        new = T.tb if tab is T.ta else T.ta
 
         def rep(a, d, q):
             s = OU[32 * a:32 * a + 32, d0:d0 + 24] if first else T.g2t[32 * a:32 * a + 32, 0:384:16]
@@ -428,18 +443,18 @@ def rank_program(g, core, T, topo):
         for a, d in ((2, 3), (3, 3), (3, 2)):
             rep(a, d, "z")
         if not first:
-            cp(u_(b0, 16), T.g2t[:].indirect(o_b), q="x")
+            cp(u_(a0, 16), T.g2t[:].indirect(o_b if hops % 2 else o_b2), q="x")
         cp(OU[0:64, f0 + 48:f0 + 96], OU[64:128, f0 + 48:f0 + 96], q="z")
-        ns = FIRST_S if first else WIDE_S
+        ns = FIRST_S
         act(new[:, 768:16 * ns], tab[:].indirect(u_(f0 + 48, ns - 48)), deps=[tok("z")], free=True)
-        if not first:
-            cp(T.g1[:], tab[:].indirect(u_(b0, 12)), q="x")
         cp(new[:, 16 * ns:NN], tab[:].indirect(u_(f0 + ns, 96 - ns)), q="z")
-        if not first:
-            tr(T.g1t[:], T.g1[:], q="x")
-            src[0:2] = [T.g1t, H]
-            wait("z", tok("x"))
-        return [tok("s"), tok("z")]
+        dep = [tok("s"), tok("z"), tok("x")]
+        for _ in range(wides - 1):
+            tab, new = new, T.tb if new is T.ta else T.ta
+            act(new[:, 0:768], tab[:].indirect(u_(f0, 48)), deps=dep)
+            cp(new[:, 768:NN], tab[:].indirect(u_(f0 + 48, 48)), dep, q="z")
+            dep = [tok("s"), tok("z"), tok("x")]
+        return new, dep
 
     def cumul(dst):
         tr(s_(wt_, 32), s_(wa, 32))
@@ -472,51 +487,42 @@ def rank_program(g, core, T, topo):
         cp(s_(y128, 64), s_(z64, 32).indirect(u_(u0_, 4)))
         tr(s_(t16, 64), s_(y128, 64))
         ts(u_(d0, 32), s_(t16, 64).indirect(o_il), -1.0, A.mult, 4096.0, A.add)
-        tab, oth = T.ta, T.tb
-        dep = rebuild(IOT, tab, True)
-        for lv, k in enumerate(LEVELS):
+        tab, dep = rebuild(IOT, True, WIDE0, 0)
+        for lv, (k, wides) in enumerate(LEVELS):
             for h in range(k):
-                hop(tab, dep, bool(lv or h))
+                hop(tab, dep, h > 0)
             doubled(tab, dep)
-            dep = rebuild(tab, oth, False)
-            tab, oth = oth, tab
+            tab, dep = rebuild(tab, False, wides, LEVELS[lv + 1][0] if lv + 1 < len(LEVELS) else TAIL)
         for h in range(TAIL):
-            hop(tab, dep)
-        cp(u_(a0, 6), T.g1t[:, 0:H:16], [tok("x")])
-        cp(u_(a0 + 6, 6), T.gyt[:, 0:H:16], [tok("z")], free=True)
+            hop(tab, dep, h > 0)
+        doubled(tab, dep)
+        o_d = u_(d0, 24)
+        cp(o_d, T.g2t[:, 0:384:16], [tok("x"), tok("z")])
         tk = tok("v")
-        for k in range(4):
-            op("s", lambda: S.activation(T.sj[:, 0:M] if k % 2 else T.sj[:, M:2 * M], T.cw[:, 160 - 32 * k:160 - 32 * k + NN].indirect(o_a), F.Copy,
-                                         accum_out=s_(kk + k, 1)), [tk], free=(k % 2 == 1))
-        cp(T.w1[:], T.cw[:, 32:32 + NN].indirect(o_a))
-        cp(T.w2[:], T.cw[:, 0:NN].indirect(o_a), free=True)
-        red(s_(kk + 4, 1), T.w1[:], A.add)
-        red(s_(kk + 5, 1), T.w2[:], A.add, free=True)
-        tt(SM[0:64, ka:ka + 6], SM[0:64, kk:kk + 6], SM[64:128, kk:kk + 6], A.add, deps=[tok("s")])
-        tt(SM[0:32, kb:kb + 6], SM[0:32, ka:ka + 6], SM[32:64, ka:ka + 6], A.add)
-        tr(SM[0:32, kt:kt + 32], SM[0:32, kb:kb + 32])
-        tt(NI[0:32, 0:16], SM[0:32, kt:kt + 16], SM[0:32, kt + 16:kt + 32], A.add)
-        ts(NI[0:32, 16:32], NI[0:32, 0:16], 4095, A.bitwise_and)
-        ts(NI[0:32, 32:48], NI[0:32, 0:16], 12, A.logical_shift_right, free=True)
-        ts(SM[0:32, kd:kd + 32], NI[0:32, 16:48], 33.0, A.min)
-        tr(SM[0:32, szw:szw + 32], SM[0:32, kd:kd + 32])
+        for k in range(2):
+            op("s", lambda: S.activation(T.g2[:] if k else T.sj[:], T.cw[:, 128 - 64 * k:128 - 64 * k + NN].indirect(o_d), F.Copy,
+                                         accum_out=s_(kk + k, 1)), [tk], free=(k == 1))
+        cp(T.g3[:, 0:384], T.cw[:, 0:NN].indirect(o_d))
+        red(s_(kk + 2, 1), T.g3[:, 0:384], A.add)
+        tt(SM[0:64, ka:ka + 3], SM[0:64, kk:kk + 3], SM[64:128, kk:kk + 3], A.add, deps=[tok("s")])
         force["v"] = True
-        for d in range(1, 4):
-            cp(SM[32 * d:32 * d + 32, szw:szw + 6], SM[0:32, szw:szw + 6], free=True)
-        cp(T.b1[:], s_(szw, 6).indirect(u_(e0, 12)))
+        for d in range(4):
+            tt(NI[32 * d:32 * d + 32, 0:3], SM[0:32, ka:ka + 3], SM[32:64, ka:ka + 3], A.add, free=True)
+        ts(NI[:, 8:14:2], NI[:, 0:3], 4095, A.bitwise_and)
+        ts(NI[:, 9:14:2], NI[:, 0:3], 12, A.logical_shift_right, free=True)
+        ts(T.b1[:], NI[:, 8:14].indirect(u_(e0, 12)), 33.0, A.min)
         tr(T.b2[:], T.b1[:])
         op("s", lambda: S.activation(T.sj[:, 0:M], T.b2[:], F.Sign, bias=col[12], accum_out=col[11]), [tok("v")])
         ts(T.b3[:], T.b2[:], col[6], A.is_equal)
-        red(s_(fcol + 1, 1), T.b3[:], A.add)
-        MS = T.ms[:, 2 * t:2 * t + 2]
-        cp(T.ms[:, 2 * t:2 * t + 1], s_(fcol + 1, 1))
-        ts(T.ms[:, 2 * t + 1:2 * t + 2], col[11], -0.5, A.mult, float(K // len(near) - M // 2), A.add, deps=[tok("s")], free=True)
+        CUM, MS = T.ms[:, 200 * t:200 * t + M], T.ms[:, 200 * t + M - 1:200 * t + M + 1]
+        scan(CUM, T.b3[:], T.b3[:], 0.0, A.add, A.max)
+        ts(T.ms[:, 200 * t + M:200 * t + M + 1], col[11], -0.5, A.mult, float(K // len(near) - M // 2), A.add, deps=[tok("s")], free=True)
         a = 32 * t + 8 * jo
         nd = spread(MS, T.lea[:, a:a + 2], "aa%d" % t, T.rm[:, 2 * t:2 * t + 2], "rm%d" % t, [tok("v")], near_first=True)
         t_aa, t_ab = [arrival("aa%d" % t, nd)], [arrival("ab%d" % t, n_far)]
         ts(s_(fcol, 1), col[11], 0.5, A.mult, float(M // 2), A.add)
         cp(T.lea[:, a:a + 2], MS, free=True)
-        scan(T.b2[:], T.b3[:], T.b3[:], s_(fcol, 1), A.add, A.max)
+        ts(T.b2[:], CUM, s_(fcol, 1), A.add)
         tt(T.b1[:], T.b2[:], T.b3[:], A.mult)
         tr(T.b2[:], T.b1[:])
         scan(T.b1[:], T.rs32[:], T.b2[:], 0.0, A.mult, A.add)
@@ -542,36 +548,39 @@ def rank_program(g, core, T, topo):
         qn, pa, la, pb, lb, rb, rc = ["%s%d" % (n, t) for n in ("qa", "pa", "la", "pb", "lb", "rb", "rc")]
         t_qa = pick(qn, 0, on, M, o_l, K)
         EA, EB = T.lea[:, 32 * t:32 * t + 32:8], T.leb[:, 8 * t:8 * t + 8:2]
-        scan(s_(pre, 4), EA, EA, 0.0, A.add, A.max, deps=t_aa)
-        red(s_(aa, 1), T.lea[:, 32 * t + 1:32 * t + 32:8], A.add, free=True)
-        ts(s_(wa + 1, 4), s_(pre, 4), s_(aa, 1), A.min, 0.0, A.max)
-        cumul(cc)
-        ts(o_p1, s_(k_i, 3), s_(cc + jo, 1), A.subtract, 0.0, A.max)
+        red(s_(aa, 1), T.lea[:, 32 * t + 1:32 * t + 32:8], A.add, deps=t_aa, free=True)
+        if jo:
+            red(col[15], T.lea[:, 32 * t:32 * t + 8 * jo:8], A.add, free=True)
+            ts(s_(wx, 32), s_(zer, 32), s_(aa, 1), A.max, col[15], A.min)
+            tr(s_(wt_, 32), s_(wx, 32))
+            red(col[15], s_(wt_, 32), A.add)
+            first_slot = col[15]
+        else:
+            first_slot = s_(zer, 1)
+        ts(o_p1, s_(k_i, 3), first_slot, A.subtract, 0.0, A.max)
         tk = pick(pa, 0, qn, K, o_p1, K, t_qa)
         eng = {offc[0]: e_off[0:4], offc[1]: e_off[4:8], peer[0]: e_on[0:4]}
         others = [(q, 12 * near.index(q)) for q in offc + peer]
         send([(cores[q], eng[q], "a1%d" % t, _q(T, pa, a, a + 12), _q(T, la, 12 * jo, 12 * jo + 12)) for q, a in others], tk[0:1])
         send([(cores[q], eng[q], "a1%d" % t, T[pa + "s"][:, a:a + 12], T[la + "s"][:, 12 * jo:12 * jo + 12]) for q, a in others], tk)
-        ts(o_p0, col[5], s_(cc + jo, 1), A.subtract, 0.0, A.max)
-        ts(s_(pre, 3), s_(cc + 1, 3), col[5], A.is_le, free=True)
+        ts(o_p0, col[5], first_slot, A.subtract, 0.0, A.max)
+        scan(s_(pre, 4), EA, EA, 0.0, A.add, A.max, free=True)
         t_a1 = [arrival("a1%d" % t, 24)] + pick(la, K, qn, K, o_p0, 16)
+        ts(s_(wa + 1, 4), s_(pre, 4), s_(aa, 1), A.min, 0.0, A.max)
+        cumul(cc)
+        ts(s_(pre, 3), s_(cc + 1, 3), col[5], A.is_le)
         tt(s_(pre, 3), s_(pre, 3), s_(stp, 3), A.mult)
         red(col[9], s_(pre, 3), A.add)
         ts(o_p2, col[9], col[4], A.add)
-        doubled(IOT, [])
         s0 = 192 * (r % 2)
         for d in range(4):
-            cp(OU[32 * d:32 * d + 32, r0:r0 + 12], T.g2t[32 * qa:32 * qa + 32, s0:s0 + 192:16], [tok("x"), tok("z")], free=True)
+            cp(OU[32 * d:32 * d + 32, r0:r0 + 12], T.g2t[32 * qa:32 * qa + 32, s0:s0 + 192:16], free=True)
         RHO = T.rho[:, M * t:M * t + M]
         act(RHO, IOT[:].indirect(o_r), deps=[tok("v")])
         t_rho = tok("s")
         dma("y", T.rt[0:1, M * t:M * t + M], T.rho[0:1, M * t:M * t + M], "out", [t_rho])
-        tk = pick(pb, 0, la, 64, o_p2, 16, t_a1)
-        a = 12 * jo
-        nd = spread(_q(T, pb, 0, 12), _q(T, lb, a, a + 12), "a2%d" % t, _q(T, rb, 0, 12), "r2%d" % t, tk[0:1])
-        spread(T[pb + "s"][:, 0:12], T[lb + "s"][:, a:a + 12], "a2%d" % t, T[rb + "s"][:, 0:12], "r3%d" % t, tk)
-        dma("y", _q(T, lb, a, a + 12), _q(T, pb, 0, 12), "o2%d" % t, tk)
-        t_a2 = [arrival("a2%d" % t, 2 * (nd + n_far)), dma("y", T[lb + "s"][:, a:a + 12], T[pb + "s"][:, 0:12], "o2%d" % t, tk)]
+        for b in range(4):
+            mm(T.pd[:, 512 * b:512 * b + M], "e", 128 * b, on, True, False, t_state, free=True)
         cp(s_(ef, 4), EA)
         cp(s_(ef + 4, 4), EB, deps=t_ab, free=True)
         scan(s_(pre, 4), EB, EB, 0.0, A.add, A.max, free=True)
@@ -581,6 +590,12 @@ def rank_program(g, core, T, topo):
         ts(col[10], s_(aa, 1), s_(ab, 1), A.add, float(-K), A.add, free=True)
         scan(s_(eg + 16, 8), s_(eg, 8), s_(eg, 8), 0.0, A.add, A.max)
         ts(s_(wa + 9, 8), s_(eg + 16, 8), col[10], A.min, 0.0, A.max)
+        tk = pick(pb, 0, la, 64, o_p2, 16, t_a1)
+        a = 12 * jo
+        nd = spread(_q(T, pb, 0, 12), _q(T, lb, a, a + 12), "a2%d" % t, _q(T, rb, 0, 12), "r2%d" % t, tk[0:1])
+        spread(T[pb + "s"][:, 0:12], T[lb + "s"][:, a:a + 12], "a2%d" % t, T[rb + "s"][:, 0:12], "r3%d" % t, tk)
+        dma("y", _q(T, lb, a, a + 12), _q(T, pb, 0, 12), "o2%d" % t, tk)
+        t_a2 = [arrival("a2%d" % t, 2 * (nd + n_far)), dma("y", T[lb + "s"][:, a:a + 12], T[pb + "s"][:, 0:12], "o2%d" % t, tk)]
         cumul(cc + 32)
         ts(s_(cc + 32, 5), s_(cc + 32, 5), float(K), A.add)
         tt(T.w3[:], RHO, IOT[:, M * r:M * r + M], A.not_equal, deps=[t_rho], free=True)
@@ -608,17 +623,6 @@ def rank_program(g, core, T, topo):
         ts(s_(f12, 12), T.w3[:, 15:M:16], 0.0, A.is_gt, float(M), A.mult, free=True)
         tt(s_(f24, 12), s_(f12, 12), s_(n_w, 12), A.add)
         cp(o_s, s_(f24, 12))
-        if t == 0:
-            for b in range(4):
-                ts(T.et[:, 512 * b + b:512 * b + 512:4], IOT[:, 0:128], pP, A.is_equal, free=True)
-            quant("e", 0, 512, T.et[:])
-            t_state = t_state + [tok("v")]
-        for b in range(4):
-            mm(T.pd[:, 512 * b:512 * b + M], "e", 128 * b, on, True, False, t_state, free=True)
-        if t + 1 < R:
-            pick("ur", 128 * (t + 1), "u", 128, o_ut[t + 1], 128)
-        else:
-            quant("w", 0, 128, T.wt[:], [t_w])
         tk = pick(rc, 0, lb, 2 * K, o_c, M, t_a2)
         tb = []
         for b in range(4):

@@ -6,34 +6,36 @@ NN = N * M
 WIDE0 = 2
 LEVELS = [(2, 2), (2, 2), (1, 1)]
 TAIL = 2
-FIRST_S = 54
+FIRST_S = 56
 HAND_ENG = 4
+KEEP, STEP = 15, 16
 C4, U8, F32, B16, I32, U16 = "float8_e4m3fn_x4", "uint8", "float32", "bfloat16", "int32", "uint16"
 
-SCRATCH = {"pd": ("psum", [128, 2048], F32), "ph": ("psum", [128, 512], F32)}
+SCRATCH = {"pd": ("psum", [128, 2048], F32), "ph": ("psum", [128, 512], F32), "pg": ("psum", [128, 512], F32)}
 for _d, _l in (
-        (B16, (("xt", 768), ("ut", 512), ("wt", 512), ("et", 2048), ("nt", 768), ("ms", 200 * R), ("lea", 32 * R), ("leb", 8 * R),
-               ("lw", 6 * R), ("lml", 48 * R), ("rm", 2 * R), ("rl", 6 * R), ("ex", NN), ("vw", NN), ("rs32", 192),
-               ("b1", 192), ("b2", 192), ("b3", 192))),
-        (F32, (("pf", 8), ("iot", NN), ("ta", NN), ("tb", NN), ("j16", 576), ("diag", 320), ("rs16", 576), ("fw", 320),
-               ("fw2", 320), ("cw", 1664), ("sm", 832), ("hs", 6 * R), ("hl", 64 * R), ("rh", 6 * R), ("mk", 576), ("g3", 576),
-               ("g3t", 576), ("sc", 832), ("ht", 192), ("g2", 384), ("g2t", 384), ("w1", 192), ("w2", 192), ("w3", 192), ("w4", 192),
-               ("sj", 384), ("rho", 192 * R), ("yb", 192), ("gy", 96), ("gyt", 96))),
-        ("float16", (("g1", 192), ("g1t", 192))),
+        (B16, (("xt", 768), ("ut", 512), ("wt", 512), ("et", 2048), ("nt", 768), ("ms", 200 * R), ("lea", 64 * R),
+               ("lw", 6 * R), ("lml", 48 * R), ("rm", 2 * R), ("rl", 6 * R), ("d32", NN), ("rs32", 384), ("m2", 384), ("b4", 384),
+               ("b5", 384), ("b1", 192), ("b2", 192), ("b3", 192), ("j4", 192), ("rs4", 192))),
+        (F32, (("pf", 8), ("iot", NN), ("ta", NN), ("tb", NN), ("j16", 576), ("diag", 512), ("rs16", 576), ("fw", 512),
+               ("fw2", 512), ("cw", 1664), ("sm", 1024), ("hs", 6 * R), ("hl", 64 * R), ("rh", 6 * R), ("mk", 576), ("g3", 576),
+               ("g3t", 576), ("sc", 832), ("ht", 192), ("ho", 192), ("g2", 384), ("g2t", 384), ("w1", 192), ("w2", 192), ("w3", 192),
+               ("sj", 384), ("rho", 192 * R), ("yb", 192), ("gy", 96), ("gyt", 96), ("cn", 136), ("nbx", 160))),
+        ("float16", (("g1", 96), ("g1t", 96))),
         (I32, (("pi", 8), ("ci", 112), ("ni", 256), ("nbw", 36))),
-        (U16, (("ou", 704), ("nbs", 16), ("nbl", 80), ("rn", 10)))):
+        (U16, (("ou", 768), ("nbs", 16), ("nbl", 40), ("rn", 5)))):
     for _n, _w in _l:
         SCRATCH[_n] = ("sbuf", [128, _w], _d)
 _mx = [("u", 128), ("ur", 384), ("w", 128), ("e", 512)] + [("on%d" % _t, 384) for _t in range(R + 1)]
 for _t in range(R):
-    _mx += [("%s%d" % (_n, _t), _w) for _n, _w in (("qa", 48), ("pa", 48), ("la", 64), ("pb", 16), ("rb", 12), ("lb", 96), ("rc", 192))]
+    _mx += [("%s%d" % (_n, _t), _w) for _n, _w in (("qa", 48), ("la", 112), ("pb", 16), ("rb", 24), ("lb", 4 * STEP), ("rc", 192))]
 for _n, _w in _mx:
     SCRATCH[_n + "q"] = ("sbuf", [128, _w], C4)
     SCRATCH[_n + "s"] = ("sbuf", [128, _w], U8)
 
-SEMAPHORES = ["v", "x", "z", "s", "p", "c", "ls", "dx", "du", "dw", "dn", "out", "an", "rn", "on"]
+ENGINE = {"v": "v", "x": "v", "z": "v", "k": "v", "s": "s", "sx": "s", "p": "p", "p1": "p", "p2": "p", "p3": "p", "c": "c"}
+SEMAPHORES = list(ENGINE) + ["ls", "dx", "du", "dw", "dn", "out", "an", "rn", "on"]
 for _t in range(R):
-    for _n in ("ah", "aa", "ab", "al", "a1", "a2", "rh", "rm", "rl", "r2", "r3", "oh", "ol", "o2"):
+    for _n in ("ah", "aa", "al", "a1", "a2", "rh", "rm", "rl", "r2", "r3", "oh", "ol"):
         SEMAPHORES.append("%s%d" % (_n, _t))
 
 A = AluOpType
@@ -72,29 +74,30 @@ def _dst(topo, dst, src):
 
 def hand_program(g, core, T, topo, plan, r, dests):
     cores = list(T.cores)
-    j = plan[r]["near"].index(r)
     engs = topo.engines(core, cores[dests[0]])
     per = len(engs) // len(dests)
     sent = [0]
 
     def fwd(src, dst, sem):
         g.remote_dma_fused([RemoteDMATransfer(dst_ids=[_dst(topo, cores[d], core)], dma_engine_mask=_mask(engs[k * per:(k + 1) * per]),
-                                              remote_sem=T.sem[sem], src=src, dst=dst) for k, d in enumerate(dests)], local_sem=T.sem.ls)
+                                              remote_sem=T.sem[sem], src=src[k % len(src)], dst=dst) for k, d in enumerate(dests)],
+                           local_sem=T.sem.ls)
         sent[0] += per * len(dests)
 
     g.wait_ge(T.sem.rn, HAND_ENG)
-    fwd(T.rn[:, 0:10], T.nbl[:, 10 * r:10 * r + 10], "an")
+    fwd([T.rn[:, 0:5]], T.nbl[:, 5 * r:5 * r + 5], "an")
+    a = 12 * r
     for t in range(R):
         g.wait_ge(T.sem["rh%d" % t], HAND_ENG)
-        fwd(T.rh[:, 6 * t:6 * t + 6], T.hl[:, 64 * t + 6 * r:64 * t + 6 * r + 6], "ah%d" % t)
-        g.wait_ge(T.sem["rm%d" % t], 2)
-        fwd(T.rm[:, 2 * t:2 * t + 2], T.leb[:, 8 * t + 2 * j:8 * t + 2 * j + 2], "ab%d" % t)
+        fwd([T.rh[:, 6 * t:6 * t + 6]], T.hl[:, 64 * t + 6 * r:64 * t + 6 * r + 6], "ah%d" % t)
+        g.wait_ge(T.sem["rm%d" % t], HAND_ENG)
+        fwd([T.rm[:, 2 * t:2 * t + 2]], T.lea[:, 64 * t + 8 * r:64 * t + 8 * r + 2], "aa%d" % t)
         g.wait_ge(T.sem["rl%d" % t], HAND_ENG)
-        fwd(T.rl[:, 6 * t:6 * t + 6], T.lml[:, 48 * t + 6 * r:48 * t + 6 * r + 6], "al%d" % t)
+        fwd([T.rl[:, 6 * t:6 * t + 6]], T.lml[:, 48 * t + 6 * r:48 * t + 6 * r + 6], "al%d" % t)
         g.wait_ge(T.sem["r2%d" % t], HAND_ENG)
-        fwd(_q(T, "rb%d" % t, 0, 12), _q(T, "lb%d" % t, 48 + 12 * j, 60 + 12 * j), "a2%d" % t)
+        fwd([_q(T, "rb%d" % t, 12 * k, 12 * k + 12) for k in range(2)], _q(T, "la%d" % t, a, a + 12), "a1%d" % t)
         g.wait_ge(T.sem["r3%d" % t], HAND_ENG)
-        fwd(T["rb%ds" % t][:, 0:12], T["lb%ds" % t][:, 48 + 12 * j:60 + 12 * j], "a2%d" % t)
+        fwd([T["rb%ds" % t][:, 12 * k:12 * k + 12] for k in range(2)], T["la%ds" % t][:, a:a + 12], "a1%d" % t)
     g.wait_ge(T.sem.ls, sent[0])
 
 
@@ -113,15 +116,15 @@ def rank_program(g, core, T, topo):
     jo = near.index(r)
     qa = r // 2
     V, S, P, Y = g.vector, g.scalar, g.tensor, g.sync
-    Q = {"v": V, "x": V, "z": V, "s": S, "p": P, "c": g, "y": Y}
-    cnt = {q: 0 for q in "vxzspc"}
-    force = {q: False for q in "vxzspc"}
+    Q = {"v": V, "s": S, "p": P, "c": g, "y": Y}
+    cnt = {q: 0 for q in ENGINE}
+    force = {q: False for q in ENGINE}
     waited = {}
     total = {}
 
     def wait(q, tok):
         name, val = tok
-        q = "v" if q in "xz" else q
+        q = ENGINE.get(q, q)
         if val > waited.get((q, name), 0):
             Q[q].wait_ge(T.sem[name], val)
             waited[(q, name)] = val
@@ -173,12 +176,12 @@ def rank_program(g, core, T, topo):
     def quant(name, a, b, src, deps=(), free=False):
         op("v", lambda: V.quantize_mx(T[name + "q"][:, a:b], T[name + "s"][:, a:b], src), deps, free)
 
-    def act(out, in_, deps=(), free=False):
-        op("s", lambda: S.activation(out, in_, F.Copy), deps, free)
+    def act(out, in_, deps=(), free=False, q="s"):
+        op(q, lambda: S.activation(out, in_, F.Copy), deps, free)
 
-    def mm(out, w, a, x, start, stop, deps, free=False):
-        op("p", lambda: P.matmul_mx(out, T[w + "q"][:, a:a + 128], T[w + "s"][:, a:a + 128], T[x + "q"][:, 0:M], T[x + "s"][:, 0:M],
-                                    start, stop), deps, free)
+    def mm(out, w, a, x, start, stop, deps, free=False, x0=0, q="p"):
+        op(q, lambda: P.matmul_mx(out, T[w + "q"][:, a:a + 128], T[w + "s"][:, a:a + 128], T[x + "q"][:, x0:x0 + M],
+                                  T[x + "s"][:, x0:x0 + M], start, stop), deps, free)
 
     def iota(out, pat, base, cm, flt=True):
         if flt:
@@ -215,9 +218,11 @@ def rank_program(g, core, T, topo):
 
     peer = [q for q in near if q != r and cores[q] in topo.cores_of(core)]
     offc = [q for q in near if q != r and q not in peer]
+    nq = offc + peer
     e_off = topo.engines(core, cores[offc[0]])
     e_on = [e for e in topo.engines(core, cores[peer[0]]) if e not in e_off]
     n_far = len(far) * (len(topo.engines(hands[0][0], cores[far[0]])) // len(hands[0][1]))
+    he, de = [e_on[0:4], e_on[4:8]], [e_off[0:2], e_off[2:4], e_off[4:6]]
     sent = [0]
 
     def send(items, deps):
@@ -227,27 +232,22 @@ def rank_program(g, core, T, topo):
                             for c, e, s, a, b in items], local_sem=T.sem.ls)
         sent[0] += sum(len(it[1]) for it in items)
 
-    def spread(src, dst, sem, hdst, hsem, deps, near_first=False, apart=False):
-        if near_first:
-            eng = [e_off[0:4], e_off[4:8], e_on[0:4], e_on[4:6], e_on[6:8]]
-        else:
-            eng = [e_off[0:2], e_off[2:4], e_off[4:6], e_on[0:4], e_on[4:8]]
-        direct = [(cores[q], eng[k], sem, src, dst) for k, q in enumerate(offc + peer)]
-        handed = [(hands[k][0], eng[3 + k], hsem, src, hdst) for k in range(2)]
+    def spread(src, dst, sem, hdst, hsem, deps, apart=False):
+        direct = [(cores[q], de[k], sem, src, dst) for k, q in enumerate(nq)]
+        handed = [(hands[k][0], he[k], hsem, src, hdst) for k in range(2)]
         if apart:
             send(handed, deps)
             send(direct, deps)
         else:
-            send(direct + handed if near_first else handed + direct, deps)
-        return 12 if near_first else 6
+            send(handed + direct, deps)
+        return 6 + n_far
 
     def arrival(sem, n):
         total[sem] = n
         return (sem, n)
 
-    half = 64 * (qa // 2)
     for k in range(4):
-        t_n = dma("y" if k % 2 == 0 else "s", T.nbw[half + 16 * k:half + 16 * k + 16, :], T.nb[:], "dn")
+        t_n = dma("y" if k % 2 == 0 else "s", T.nbw[16 * k:16 * k + 16, :], T.nb[:], "dn")
     t_x = dma("y", T.xt[:], T.x[:], "dx")
     t_u = dma("s", T.ut[:], T.u[:], "du")
     t_w = dma("y", T.wt[:], T.w[:], "dw")
@@ -260,175 +260,218 @@ def rank_program(g, core, T, topo):
     iota(T.ci[:, 0:96], [[1, 48], [0, 2]], 0, 0, flt=False)
     iota(T.ci[:, 96:104], [[16, 4], [0, 2]], 0, 0, flt=False)
     t_c1 = tok("c")
-    for k in range(1, 6):
-        op("s", lambda: S.activation(IOT[:, 256 * k:256 * k + 256], IOT[:, 0:256], F.Identity, bias=float(256 * k)), [t_p], free=True)
 
-    mset(T.nbw[64 - half:128 - half, :], 0)
     PI, PF = T.pi, T.pf
+    c0 = sm(24)
+    col = [s_(c0 + k, 1) for k in range(24)]
+    place = [0, 2, 1, 3]
+    for a in range(4):
+        mset(SM[32 * a:32 * a + 32, c0 + 1:c0 + 2], float(5 * place[a ^ qa]))
     ts(PI[:, 1:2], PI[:, 0:1], 15, A.bitwise_and, deps=[t_p0], free=True)
     ts(PI[:, 2:3], PI[:, 0:1], 4, A.logical_shift_right, 1, A.bitwise_and, free=True)
     ts(PI[:, 3:4], PI[:, 0:1], 5, A.logical_shift_right, free=True)
-    ts(PI[:, 4:5], PI[:, 0:1], 1, A.bitwise_and, free=True)
+    ts(PI[:, 4:5], PI[:, 0:1], 7, A.bitwise_and, free=True)
     ts(PI[:, 5:6], PI[:, 0:1], 31, A.bitwise_and, free=True)
-    cp(PF[:, 0:6], PI[:, 0:6])
-    pP, pI, pS, pA, pO, pR = [PF[:, k:k + 1] for k in range(6)]
-    c0 = sm(16)
-    col = [s_(c0 + k, 1) for k in range(16)]
-    tt(col[0], pI, pS, A.add)
-    ts(col[1], pA, float(qa), A.not_equal, 20.0, A.mult, free=True)
-    ts(col[0], col[0], 2.0, A.mult, pO, A.subtract)
+    ts(PI[:, 6:7], PI[:, 0:1], 2, A.logical_shift_right, 3, A.bitwise_and, free=True)
+    cp(PF[:, 0:7], PI[:, 0:7])
+    pP, pI, pS, pA, p8, pR, pQ = [PF[:, k:k + 1] for k in range(7)]
+    ts(NI[:, 0:1], pI, col[1], A.add)
+    ts(NI[:, 1:2], NI[:, 0:1], 1, A.bitwise_and)
+    ts(col[0], NI[:, 0:1], pS, A.add, 2.0, A.mult, free=True)
+    tt(col[0], col[0], NI[:, 1:2], A.subtract)
     o_nb = ou(1)
-    ts(o_nb, col[0], col[1], A.add, 35.0, A.min)
+    ts(o_nb, col[0], 35.0, A.min)
     o_ut = [ou(8) for _ in range(R)]
     for t in range(R):
         mset(o_ut[t], t)
-    cp(T.nbs[:], T.nbw[:, 0:36].indirect(o_nb), deps=[t_n])
+    cp(T.nbw[64:128, :], T.nbw[0:64, :], deps=[t_n], free=True)
+    cp(T.nbs[:], T.nbw[:, 0:36].indirect(o_nb))
     t_nbs = tok("v")
-    nd = spread(T.nbs[:, 0:10], T.nbl[:, 10 * r:10 * r + 10], "an", T.rn[:, 0:10], "rn", [t_nbs], apart=True)
-    t_an = [arrival("an", nd + n_far), dma("y", T.nbl[:, 10 * r:10 * r + 10], T.nbs[:, 0:10], "on", [t_nbs])]
+    nd = spread(T.nbs[:, 0:5], T.nbl[:, 5 * r:5 * r + 5], "an", T.rn[:, 0:5], "rn", [t_nbs], apart=True)
+    t_an = [arrival("an", nd), dma("y", T.nbl[:, 5 * r:5 * r + 5], T.nbs[:, 0:5], "on", [t_nbs])]
 
     quant("u", 0, 128, T.ut[:], [t_u])
     t_ur = pick("ur", 0, "u", 128, o_ut[0], 128)
     quant("on0", 0, M, T.xt[:], [t_x], free=True)
     t_state = [tok("v")]
 
-    def heights(t, deps):
-        mm(T.ph[:, 0:M], "ur", 128 * t, "on%d" % t, True, True, deps)
-        tr(T.ht[:], T.ph[:, 0:M], deps=[tok("p")])
+    def send_heights(t):
         HS = T.hs[:, 6 * t:6 * t + 6]
-        cp(HS, T.ht[:, 0:M:32])
         tk = tok("v")
         a = 64 * t + 6 * r
-        nd = spread(HS, T.hl[:, a:a + 6], "ah%d" % t, T.rh[:, 6 * t:6 * t + 6], "rh%d" % t, [tk])
-        return [arrival("ah%d" % t, nd + n_far), dma("y", T.hl[:, a:a + 6], HS, "oh%d" % t, [tk])]
+        nd = spread(HS, T.hl[:, a:a + 6], "ah%d" % t, T.rh[:, 6 * t:6 * t + 6], "rh%d" % t, [tk], apart=True)
+        return [arrival("ah%d" % t, nd), dma("y", T.hl[:, a:a + 6], HS, "oh%d" % t, [tk])]
 
-    for k in range(1, 6):
-        act(T.j16[:, 96 * k:96 * k + 96], T.j16[:, 0:96], free=True)
+    def numbers(a, n):
+        op("s", lambda: S.activation(IOT[:, a:a + n], IOT[:, 0:n], F.Identity, bias=float(a)), [t_p], free=(a != 512))
+
+    numbers(256, 256)
+    numbers(512, 512)
+    tk = tok("s")
+    for k in range(2):
+        op("sx", lambda: S.activation(T.et[:, 1024 * k:1024 * k + 1024], IOT[:, 0:1024], F.Copy, scale=0.0), [tk], free=True)
+    t_et = tok("sx")
+    numbers(1024, 512)
+    for a, n in ((96, 96), (192, 192), (384, 192)):
+        act(T.j16[:, a:a + n], T.j16[:, 0:n], free=(a != 192))
     t_iot = tok("s")
-    t_h = heights(0, t_state + t_ur)
+    mm(T.ph[:, 0:M], "ur", 0, "on0", True, True, t_state + t_ur)
+    tr(T.ht[:], T.ph[:, 0:M], deps=[tok("p")])
+    cp(T.hs[:, 0:6], T.ht[:, 0:M:32])
+    t_h = send_heights(0)
 
+    k_n, n_f, n_w, n_o, n_id = sm(3), sm(8), sm(12), sm(12), sm(48)
+    CN = T.cn
+    r8, dl, tb0, ones, stp = 0, 32, 64, 96, 128
     iota(T.fw[:, 0:48], [[0, 4], [1, 12]], 0, 0)
-    iota(T.fw[:, 48:84], [[6, 3], [10, 2], [1, 6]], 0, 0)
+    iota(T.fw[:, 48:84], [[6, 3], [5, 2], [1, 6]], 0, 0)
     iota(T.fw2[:, 0:36], [[6, 3], [0, 2], [1, 6]], 0, 0)
+    iota(T.fw[:, 84:96], [[0, 12]], 0, 0)
     iota(T.fw[:, 96:112], [[64, 8], [16, 2]], 0, 0)
-    iota(T.fw[:, 144:192], [[1, 8], [0, 6]], 40, 0)
-    iota(T.fw[:, 192:240], [[1, 8], [0, 6]], 41, 0)
+    iota(T.fw[:, 112:144], [[0, 32]], 0, 0)
+    iota(T.fw[:, 144:240], [[0, 2], [1, 8], [0, 6]], 24, 0)
     iota(T.fw[:, 288:320], [[1, 16], [32, 2]], 0, 0)
+    for c in range(4):
+        iota(T.fw[:, 240 + 12 * c:252 + 12 * c], [[-8, 12]], M - 2 - 2 * ((c - jo) % 4), 0)
+    iota(T.fw[:, 320:512], [[1, 8], [0, 6], [8, 4]], 0, 0)
     t_c2 = tok("c")
-    for out, n in ((T.cw[:, 0:832], 832), (T.cw[:, 832:1664], 832), (T.et[:, 0:1024], 1024), (T.et[:, 1024:2048], 1024)):
-        op("s", lambda: S.activation(out, IOT[:, 0:n], F.Copy, scale=0.0))
-    t_zero = tok("s")
-    mset(SM[:, 16:832], 0.0)
+    iota(T.j4[:], [[0, 48], [1, 4]], 0, 0)
     for t in range(R):
-        mset(T.hl[:, 64 * t + 48:64 * t + 64], 0.0)
-    ts(T.diag[:], T.j16[:, 0:320], pI, A.is_equal, deps=[t_c1, t_iot])
-    ts(T.rs16[:], T.j16[:], 0.0, A.is_gt, free=True)
-    mset(T.fw[:, 84:96], 0.0)
-    mset(T.fw[:, 112:128], 0.0)
-    mset(T.fw[:, 136:144], 0.0)
-    order = near + far
+        iota(T.hl[:, 64 * t + 48:64 * t + 64], [[0, 16]], 0, 0)
+    iota(T.b4[:], [[0, 12], [1, 32]], 0, 0)
+    t_c3 = tok("c")
+    spot = [2 * K if q == r else 12 * q for q in range(N)]
     for q in range(N):
-        mset(T.fw[:, 240 + 6 * q:246 + 6 * q], float(near.index(q) if q in near else 32 + far.index(q)))
-        mset(T.fw[:, 128 + q:129 + q], float(order.index(q)))
-    o_b, o_b2, o_own = ou(1), ou(1), ou(1)
+        turn = plan[q]["near"].index(q)
+        for c in range(4):
+            iota(CN[:, dl + 8 * c + q:dl + 8 * c + q + 1], [[0, 1]], 3 - (c - turn) % 4, 0)
+            iota(CN[:, tb0 + 8 * c + q:tb0 + 8 * c + q + 1], [[0, 1]], STEP * c + 1 - int(c < turn), 0)
+        if q + 1 < N:
+            iota(CN[:, stp + q:stp + q + 1], [[0, 1]], spot[q + 1] - spot[q], 0)
+    for c in range(4):
+        iota(CN[:, r8 + 8 * c:r8 + 8 * c + 7], [[0, 7]], 1, 0)
+        iota(CN[:, r8 + 8 * c + 7:r8 + 8 * c + 8], [[0, 1]], 0, 0)
+    iota(CN[:, ones:ones + 32], [[0, 32]], 1, 0)
+    t_c4 = tok("c")
+    op("s", lambda: S.activation(T.rs16[:], T.j16[:], F.Sign), free=True)
+    t_rs = tok("s")
+    for k in range(2):
+        op("s", lambda: S.activation(T.cw[:, 832 * k:832 * k + 832], IOT[:, 0:832], F.Copy, scale=0.0), free=True)
+    t_zero = tok("s")
+    ts(T.d32[:, 0:32], IOT[:, 0:32], pR, A.is_equal, deps=[t_p])
+    tk = tok("v")
+    for k in (32, 64, 128, 256, 512):
+        act(T.d32[:, k:2 * k], T.d32[:, 0:k], [tk])
+    act(T.d32[:, 1024:NN], T.d32[:, 0:512], free=True)
+    z64, y128, t16, m24, m12, e48, f24, f12 = sm(64), sm(128), sm(128), sm(24), sm(16), sm(48), sm(24), sm(32)
+    kk, ka, cc, mj, wa, exc, ne = sm(8), sm(8), sm(32), sm(32), sm(32), sm(40), sm(16)
+    m32, om = sm(16), sm(16)
+    mset(s_(ne, 16), 0.0)
+    mset(s_(f12, 32), 0.0)
+    mset(s_(wa, 40), 0.0)
+    o_b, o_b2, o_own, o_n0, o_n1, o_d4 = ou(1), ou(1), ou(1), ou(2), ou(2), ou(12)
     u0_, e0 = take("ou", 8), take("ou", 96)
     o_dup = u_(u0_, 8)
-    k_i, k_n, n_f, n_w, n_id, ones, stp, zer = sm(3), sm(3), sm(6), sm(12), sm(48), sm(32), sm(3), sm(32)
     ts(col[2], pS, 32.0, A.mult, free=True)
     ts(col[3], pA, 12.0, A.mult, free=True)
     ts(col[13], pI, 11.0, A.min, 32.0, A.mult, free=True)
     ts(col[14], pS, 16.0, A.mult, free=True)
-    spot = [K if j == jo else 12 * j for j in range(4)]
-    ts(col[4], pI, 11.0, A.min, float(spot[0]), A.add, free=True)
-    ts(col[5], pI, 11.0, A.min, float(12 * jo), A.add, free=True)
+    ts(col[4], pA, 10.0, A.mult, free=True)
     ts(col[6], pR, 2.0, A.add, free=True)
     ts(col[12], pR, 2.5, A.add, -1.0, A.mult, free=True)
     ts(col[7], pA, 384.0, A.mult, pR, A.add, free=True)
-    cp(u_(e0, 96), T.ci[:, 0:96], free=True)
+    cp(u_(e0, 12), T.ci[:, 0:12], [t_c1], free=True)
     ts(o_dup, T.ci[:, 96:104], pI, A.add, free=True)
-    ts(s_(k_i, 3), IOT[:, 0:48:16], pI, A.add, free=True)
-    ts(s_(n_f, 6), IOT[:, 0:192:32], pR, A.add, 1.0 / 1024, A.mult, free=True)
+    for o, k in ((o_n0, 0), (o_n1, 1)):
+        ts(o, s_(f12, 2), p8, A.add, float(k), A.add, free=(k == 1))
+    ts(o_d4, IOT[:, 0:48:4], pQ, A.add, free=True)
+    ts(s_(n_f, 6), IOT[:, 0:192:32], pR, A.add, 1.0 / 256, A.mult, free=True)
     ts(s_(n_w, 12), IOT[:, 0:192:16], pI, A.add, free=True)
-    mset(s_(ones, 32), 1.0)
-    mset(T.rs32[:], 1.0)
-    for j in range(3):
-        mset(s_(stp + j, 1), float(spot[j + 1] - spot[j]))
-    ts(T.fw2[:, 0:36], T.fw2[:, 0:36], 10.0, A.is_ge, 10.0, A.mult, deps=[t_c2], free=True)
-    tt(T.fw[:, 48:84], T.fw[:, 48:84], T.fw2[:, 0:36], A.add)
+    ts(s_(n_o, 12), s_(n_w, 12), float(M * r), A.add)
+    o_p0, o_x, o_e = ou(1), ou(1), ou(12)
+    ts(col[5], pI, 5.0, A.min, 2.0, A.mult, free=True)
+    ts(o_e, T.ci[:, 0:12], 32.0, A.mult, 31.0, A.add, free=True)
+    ts(col[15], pI, float(spot[0]), A.add, free=True)
+    ts(o_p0, pI, 11.0, A.min, float(12 * jo), A.add, free=True)
     ts(o_own, pI, 11.0, A.min, col[3], A.add, free=True)
     ts(o_b2, col[13], col[14], A.add, free=True)
-    ts(s_(k_n, 3), s_(k_i, 3), 1.0, A.add, -1.0, A.mult, free=True)
-    mset(T.rs32[:, 0:192:32], 0.0)
+    ts(o_x, col[5], pS, A.add)
+    cp(T.w3[:], s_(n_f, 6).indirect(u_(e0, 12)), free=True)
+    for b in range(4):
+        ts(T.et[:, 512 * b + b:512 * b + 512:4], IOT[:, 0:128], pP, A.is_equal, deps=[t_et], free=True)
+    quant("e", 0, 512, T.et[:])
+    t_state = t_state + [tok("v")]
+    ts(T.diag[:], T.j16[:, 0:512], pI, A.is_equal, deps=[t_iot], free=True)
     ts(s_(n_id + 36, 12), IOT[:, 0:384:32], col[7], A.add, free=True)
+    for k in range(1, 4):
+        ts(T.fw2[:, 48 * k:48 * k + 36], T.fw2[:, 0:36], 5.0 * k, A.is_ge, 35.0, A.mult, deps=[t_c2], free=True)
+    for k in range(1, 4):
+        tt(T.fw[:, 48:84], T.fw[:, 48:84], T.fw2[:, 48 * k:48 * k + 36], A.add)
     tt(T.fw2[:], T.fw[:], T.diag[:], A.mult)
-    scan(T.fw[:], T.rs16[:, 0:320], T.fw2[:], 0.0, A.mult, A.add)
-    o_m, o_nbf, o_eg, o_lo, o_hi, o_of, o_il = ou(3), ou(3), ou(1), ou(3), ou(3), ou(3), ou(2)
+    scan(T.fw[:], T.rs16[:, 0:512], T.fw2[:], 0.0, A.mult, A.add, deps=[t_rs])
+    o_m, o_nbf, o_va, o_il, o_tb = ou(3), ou(3), ou(3), ou(2), ou(12)
     force["v"] = True
-    for dst, a, n in ((o_m, 0, 3), (o_nbf, 3, 3), (o_eg, 8, 1), (o_lo, 9, 3), (o_hi, 12, 3), (o_of, 15, 3), (o_il, 18, 2)):
+    for dst, a, n in ((o_m, 0, 3), (o_va, 9, 3), (s_(k_n, 3), 15, 3), (o_il, 18, 2), (o_tb, 20, 12)):
         cp(dst, T.fw[:, 16 * a + 15:16 * (a + n):16], free=True)
+    ts(o_nbf, T.fw[:, 63:96:16], col[4], A.add, free=True)
     ts(o_b, T.fw[:, 111:112], col[2], A.add, 383.0, A.min, free=True)
     x0 = 128 + M * r
     ts(T.cw[:, x0:x0 + 32], IOT[:, 0:32], pR, A.is_equal, deps=[t_zero], free=True)
     ts(T.cw[:, x0 + 32:x0 + 64], IOT[:, 0:32], pR, A.is_equal, 4096.0, A.mult, free=True)
-    for b in range(4):
-        ts(T.et[:, 512 * b + b:512 * b + 512:4], IOT[:, 0:128], pP, A.is_equal, free=True)
-    quant("e", 0, 512, T.et[:])
-    t_state = t_state + [tok("v")]
-    for t in range(1, R):
-        pick("ur", 128 * t, "u", 128, o_ut[t], 128)
-    quant("w", 0, 128, T.wt[:], [t_w])
+    t_ur = pick("ur", 128, "u", 128, o_ut[1], 128)
+    ts(T.rs4[:], T.j4[:], 0.0, A.is_gt, deps=[t_c3], free=True)
+    ts(T.rs32[:], T.b4[:], 0.0, A.is_gt, free=True)
 
-    nbx = sm(40)
+    NB = T.nbx
+    cp(NB[:, 0:40], T.nbl[:], deps=t_an, free=True)
+    cp(NB[0:64, 40:80], T.nbl[64:128, :], free=True)
+    cp(NB[64:128, 40:80], T.nbl[0:64, :], free=True)
+    force["v"] = True
     for a in range(4):
-        for part in range(2):
-            s0 = 32 * (a ^ part)
-            cp(SM[32 * a:32 * a + 32, nbx + 20 * part:nbx + 20 * part + 20], T.nbl[s0:s0 + 32, 20 * a:20 * a + 20], deps=t_an, free=True)
-    cp(NI[:, 0:48], s_(nbx, 40).indirect(o_nbf))
-    o_nh, o_nl, o_nn = ou(36), take("ou", 36), ou(36)
+        cp(NB[32 * a:32 * a + 32, 80:160], NB[32 * (a ^ 1):32 * (a ^ 1) + 32, 0:80], free=True)
+    cp(NI[:, 0:48], NB[:].indirect(o_nbf))
+    o_nh, o_nl, o_nn = ou(36), ou(36), ou(36)
     ts(NI[:, 192:228], NI[:, 0:36], 15, A.bitwise_and)
     cp(o_nn, NI[:, 0:36], free=True)
-    cp(u_(o_nl, 36), NI[:, 192:228])
-    act(T.mk[:, 0:384], T.diag[:, 0:16].indirect(u_(o_nl, 24)), deps=[tok("v")])
+    cp(o_nl, NI[:, 192:228])
+    act(T.mk[:], T.diag[:, 0:16].indirect(o_nl), deps=[tok("v")])
     t_mk = tok("s")
     act(T.g3t[:], IOT[:].indirect(o_nn))
     t_id = tok("s")
-    ts(NI[:, 48:84], NI[:, 0:36], 10, A.logical_shift_right)
-    ts(NI[:, 96:132], NI[:, 0:36], 4, A.logical_shift_right, 1, A.bitwise_and, free=True)
+    ts(NI[:, 48:84], NI[:, 0:36], 1024, A.bitwise_and, 4, A.logical_shift_right)
+    ts(NI[:, 96:132], NI[:, 0:36], 16, A.bitwise_and, free=True)
     ts(NI[:, 144:180], NI[:, 0:36], 5, A.logical_shift_right, 31, A.bitwise_and, free=True)
-    ts(NI[:, 48:84], NI[:, 48:84], 2.0, A.mult)
-    cp(T.mk[:, 384:576], T.diag[:, 0:16].indirect(u_(o_nl + 24, 12)), free=True)
     tt(NI[:, 48:84], NI[:, 48:84], NI[:, 96:132], A.add)
-    ts(NI[:, 48:84], NI[:, 48:84], 32.0, A.mult)
+    tt(NI[:, 144:180], NI[:, 144:180], NI[:, 96:132], A.add, free=True)
     tt(NI[:, 48:84], NI[:, 48:84], NI[:, 144:180], A.add)
     cp(o_nh, NI[:, 48:84])
 
-    z64, y128, t16, m24, m12, e48, f24, f12 = sm(64), sm(128), sm(128), sm(24), sm(16), sm(48), sm(24), sm(32)
-    kk, ka, wa, cc = sm(8), sm(8), sm(32), sm(64)
-    fcol, enc, lmin = m12, f12, f24
-    wt_, wx, pre, aa, ab, ef, eg = y128 + 32, y128 + 64, m24, m24 + 8, m24 + 9, f24, e48
-    o_l, o_p0, o_p1, o_p2, o_c, o_s = ou(3), ou(1), ou(3), ou(1), ou(12), ou(12)
-    a0, r0, d0, f0 = take("ou", 16), take("ou", 12), take("ou", 32), take("ou", 96)
-    o_a, o_r = u_(a0, 12), u_(r0, 12)
+    lmin = f24
+    wt_, wx, pre, aa = y128 + 32, y128 + 64, m24, m24 + 16
+    o_l, o_p2, o_c, o_s, o_r = ou(3), ou(1), ou(12), ou(12), ou(12)
+    a0, d0, f0, h2, r2 = take("ou", 16), take("ou", 32), take("ou", 96), take("ou", 24), take("ou", 24)
+    o_a = u_(a0, 12)
     H = M // 2
+    rf = 176
 
-    def hop(tab, deps, conv=True):
+    def hop(tab, deps, conv):
         if conv:
-            cp(u_(a0, 6), T.g1t[:, 0:H:16], q="x")
             cp(u_(a0 + 6, 6), T.gyt[:, 0:H:16], q="z")
+            cp(u_(a0, 6), T.g1t[:, 0:H:16], q="x")
         act(T.gy[:], tab[:].indirect(u_(a0 + 6, 6)), deps=[tok("z")] + deps)
-        cp(T.g1[:, 0:H], tab[:].indirect(u_(a0, 6)), deps, q="x")
-        tr(T.g1t[:, 0:H], T.g1[:, 0:H], q="x")
+        cp(T.g1[:], tab[:].indirect(u_(a0, 6)), deps, q="x")
         tr(T.gyt[:], T.gy[:], [tok("s")], q="z")
+        tr(T.g1t[:], T.g1[:], q="x")
 
     def doubled(tab, deps):
-        cp(u_(d0, 12), T.g1t[:, 0:H:8], q="x")
         cp(u_(d0 + 12, 12), T.gyt[:, 0:H:8], q="z")
+        cp(u_(d0, 12), T.g1t[:, 0:H:8], q="x")
         act(T.g2[:, 192:384], tab[:].indirect(u_(d0 + 12, 12)), deps=[tok("z")] + deps)
         cp(T.g2[:, 0:192], tab[:].indirect(u_(d0, 12)), deps, q="x")
-        tr(T.g2t[:, 0:192], T.g2[:, 0:192], q="x")
         tr(T.g2t[:, 192:384], T.g2[:, 192:384], [tok("s")], q="z")
+        tr(T.g2t[:, 0:192], T.g2[:, 0:192], q="x")
 
-    def rebuild(tab, first, wides, hops):
+    def rebuild(tab, first, wides, ahead):
         both = [tok("x"), tok("z"), tok("v")]
         new = T.tb if tab is T.ta else T.ta
 
@@ -439,27 +482,27 @@ def rank_program(g, core, T, topo):
             rep(a, d, "x")
         rep(2, 2, "z")
         cp(OU[64:128, f0:f0 + 48], OU[0:64, f0:f0 + 48], q="x")
-        act(new[:, 0:768], tab[:].indirect(u_(f0, 48)), deps=[tok("x")])
+        act(new[:, 0:768], tab[:].indirect(u_(f0, 48)), deps=[tok("x")], q="sx")
         for a, d in ((2, 3), (3, 3), (3, 2)):
             rep(a, d, "z")
         if not first:
-            cp(u_(a0, 16), T.g2t[:].indirect(o_b if hops % 2 else o_b2), q="x")
+            cp(u_(a0, 16), T.g2t[:].indirect(o_b if ahead % 2 else o_b2), both, q="k")
         cp(OU[0:64, f0 + 48:f0 + 96], OU[64:128, f0 + 48:f0 + 96], q="z")
         ns = FIRST_S
-        act(new[:, 768:16 * ns], tab[:].indirect(u_(f0 + 48, ns - 48)), deps=[tok("z")], free=True)
+        act(new[:, 768:16 * ns], tab[:].indirect(u_(f0 + 48, ns - 48)), deps=[tok("z")], free=True, q="sx")
         cp(new[:, 16 * ns:NN], tab[:].indirect(u_(f0 + ns, 96 - ns)), q="z")
-        dep = [tok("s"), tok("z"), tok("x")]
+        dep = [tok("sx"), tok("z"), tok("x"), tok("k")]
         for _ in range(wides - 1):
             tab, new = new, T.tb if new is T.ta else T.ta
-            act(new[:, 0:768], tab[:].indirect(u_(f0, 48)), deps=dep)
+            act(new[:, 0:768], tab[:].indirect(u_(f0, 48)), deps=dep, q="sx")
             cp(new[:, 768:NN], tab[:].indirect(u_(f0 + 48, 48)), dep, q="z")
-            dep = [tok("s"), tok("z"), tok("x")]
+            dep = [tok("sx"), tok("z"), tok("x"), tok("k")]
         return new, dep
 
     def cumul(dst):
         tr(s_(wt_, 32), s_(wa, 32))
         red(col[8], s_(wt_, 32), A.add)
-        ts(s_(wx, 32), s_(ones, 32), col[8], A.mult)
+        ts(s_(wx, 32), CN[:, ones:ones + 32], col[8], A.mult)
         tr(s_(dst, 32), s_(wx, 32))
 
     for t in range(R):
@@ -504,6 +547,9 @@ def rank_program(g, core, T, topo):
                                          accum_out=s_(kk + k, 1)), [tk], free=(k == 1))
         cp(T.g3[:, 0:384], T.cw[:, 0:NN].indirect(o_d))
         red(s_(kk + 2, 1), T.g3[:, 0:384], A.add)
+        s0 = 192 * (r % 2)
+        for d in (0, 1):
+            cp(NI[32 * d:32 * d + 32, rf:rf + 12], T.g2t[32 * qa:32 * qa + 32, s0:s0 + 192:16], free=True)
         tt(SM[0:64, ka:ka + 3], SM[0:64, kk:kk + 3], SM[64:128, kk:kk + 3], A.add, deps=[tok("s")])
         force["v"] = True
         for d in range(4):
@@ -516,126 +562,134 @@ def rank_program(g, core, T, topo):
         ts(T.b3[:], T.b2[:], col[6], A.is_equal)
         CUM, MS = T.ms[:, 200 * t:200 * t + M], T.ms[:, 200 * t + M - 1:200 * t + M + 1]
         scan(CUM, T.b3[:], T.b3[:], 0.0, A.add, A.max)
-        ts(T.ms[:, 200 * t + M:200 * t + M + 1], col[11], -0.5, A.mult, float(K // len(near) - M // 2), A.add, deps=[tok("s")], free=True)
-        a = 32 * t + 8 * jo
-        nd = spread(MS, T.lea[:, a:a + 2], "aa%d" % t, T.rm[:, 2 * t:2 * t + 2], "rm%d" % t, [tok("v")], near_first=True)
-        t_aa, t_ab = [arrival("aa%d" % t, nd)], [arrival("ab%d" % t, n_far)]
-        ts(s_(fcol, 1), col[11], 0.5, A.mult, float(M // 2), A.add)
-        cp(T.lea[:, a:a + 2], MS, free=True)
-        ts(T.b2[:], CUM, s_(fcol, 1), A.add)
+        t_gt = tok("s")
+        op("s", lambda: S.activation(T.ms[:, 200 * t + M:200 * t + M + 1], col[11], F.Identity, bias=float(K // N - M // 2), scale=-0.5))
+        t_ms = tok("s")
+        a = 64 * t + 8 * r
+        nd = spread(MS, T.lea[:, a:a + 2], "aa%d" % t, T.rm[:, 2 * t:2 * t + 2], "rm%d" % t, [tok("v"), t_ms])
+        t_aa = [arrival("aa%d" % t, nd)]
+        ts(T.b2[:], CUM, 2.0, A.mult, col[11], A.add, deps=[t_gt])
         tt(T.b1[:], T.b2[:], T.b3[:], A.mult)
         tr(T.b2[:], T.b1[:])
-        scan(T.b1[:], T.rs32[:], T.b2[:], 0.0, A.mult, A.add)
-        tt(s_(enc, 6), T.b1[:, 31:M:32], s_(n_f, 6), A.add)
+        scan(T.b1[:], T.rs32[:, 0:M], T.b2[:], 0.0, A.mult, A.add)
         LW = T.lw[:, 6 * t:6 * t + 6]
-        cp(LW, T.b1[:, 31:M:32], free=True)
-        tk = tok("v")
+        op("s", lambda: S.activation(LW, T.b1[:, 31:M:32], F.Identity, bias=float(M // 2 - 1 + jo), scale=0.5), [tok("v")])
+        t_lw = tok("s")
         a = 48 * t + 6 * r
-        nd = spread(LW, T.lml[:, a:a + 6], "al%d" % t, T.rl[:, 6 * t:6 * t + 6], "rl%d" % t, [tk])
-        t_al = [arrival("al%d" % t, nd + n_far), dma("y", T.lml[:, a:a + 6], LW, "ol%d" % t, [tk])]
-        cp(T.w2[:], s_(enc, 6).indirect(u_(e0, 12)))
+        nd = spread(LW, T.lml[:, a:a + 6], "al%d" % t, T.rl[:, 6 * t:6 * t + 6], "rl%d" % t, [t_lw])
+        t_al = [arrival("al%d" % t, nd), dma("y", T.lml[:, a:a + 6], LW, "ol%d" % t, [t_lw])]
+        tt(T.w2[:], T.b1[:].indirect(o_e), T.w3[:], A.add)
         tr(T.w1[:], T.w2[:])
         tk = tok("v")
         tks = []
-        for c in range(2):
-            op("s", lambda: S.activation(T.sj[:, M * c:M * c + M], T.w1[:], F.Abs, bias=s_(k_n + c, 1)), [tk])
-            tks.append(tok("s"))
+        for c, q in enumerate(("s", "sx")):
+            op(q, lambda: S.activation(T.sj[:, M * c:M * c + M], T.w1[:], F.Abs, bias=s_(k_n + c, 1)), [tk], free=True)
+            tks.append(tok(q))
         ts(T.w2[:], T.w1[:], s_(k_n + 2, 1), A.add)
         op("v", lambda: V.tensor_reduce(s_(lmin + 2, 1), T.w2[:], X, A.min, apply_absolute_value=True))
         for c in range(2):
             red(s_(lmin + c, 1), T.sj[:, M * c:M * c + M], A.min, deps=[tks[c]], free=True)
-        ts(o_l, s_(lmin, 3), 1024.0, A.mult, float(M - 1), A.min)
-        qn, pa, la, pb, lb, rb, rc = ["%s%d" % (n, t) for n in ("qa", "pa", "la", "pb", "lb", "rb", "rc")]
-        t_qa = pick(qn, 0, on, M, o_l, K)
-        EA, EB = T.lea[:, 32 * t:32 * t + 32:8], T.leb[:, 8 * t:8 * t + 8:2]
-        red(s_(aa, 1), T.lea[:, 32 * t + 1:32 * t + 32:8], A.add, deps=t_aa, free=True)
-        if jo:
-            red(col[15], T.lea[:, 32 * t:32 * t + 8 * jo:8], A.add, free=True)
-            ts(s_(wx, 32), s_(zer, 32), s_(aa, 1), A.max, col[15], A.min)
-            tr(s_(wt_, 32), s_(wx, 32))
-            red(col[15], s_(wt_, 32), A.add)
-            first_slot = col[15]
-        else:
-            first_slot = s_(zer, 1)
-        ts(o_p1, s_(k_i, 3), first_slot, A.subtract, 0.0, A.max)
-        tk = pick(pa, 0, qn, K, o_p1, K, t_qa)
-        eng = {offc[0]: e_off[0:4], offc[1]: e_off[4:8], peer[0]: e_on[0:4]}
-        others = [(q, 12 * near.index(q)) for q in offc + peer]
-        send([(cores[q], eng[q], "a1%d" % t, _q(T, pa, a, a + 12), _q(T, la, 12 * jo, 12 * jo + 12)) for q, a in others], tk[0:1])
-        send([(cores[q], eng[q], "a1%d" % t, T[pa + "s"][:, a:a + 12], T[la + "s"][:, 12 * jo:12 * jo + 12]) for q, a in others], tk)
-        ts(o_p0, col[5], first_slot, A.subtract, 0.0, A.max)
-        scan(s_(pre, 4), EA, EA, 0.0, A.add, A.max, free=True)
-        t_a1 = [arrival("a1%d" % t, 24)] + pick(la, K, qn, K, o_p0, 16)
-        ts(s_(wa + 1, 4), s_(pre, 4), s_(aa, 1), A.min, 0.0, A.max)
-        cumul(cc)
-        ts(s_(pre, 3), s_(cc + 1, 3), col[5], A.is_le)
-        tt(s_(pre, 3), s_(pre, 3), s_(stp, 3), A.mult)
-        red(col[9], s_(pre, 3), A.add)
-        ts(o_p2, col[9], col[4], A.add)
-        s0 = 192 * (r % 2)
-        for d in range(4):
-            cp(OU[32 * d:32 * d + 32, r0:r0 + 12], T.g2t[32 * qa:32 * qa + 32, s0:s0 + 192:16], free=True)
-        RHO = T.rho[:, M * t:M * t + M]
-        act(RHO, IOT[:].indirect(o_r), deps=[tok("v")])
-        t_rho = tok("s")
-        dma("y", T.rt[0:1, M * t:M * t + M], T.rho[0:1, M * t:M * t + M], "out", [t_rho])
+        ts(o_l, s_(lmin, 3), 256.0, A.mult, float(M - 1), A.min)
+        qn, la, pb, lb, rb, rc = ["%s%d" % (n, t) for n in ("qa", "la", "pb", "lb", "rb", "rc")]
+        tk = pick(qn, 0, on, M, o_l, K, t_state)
+        a = 12 * r
+        send([(hands[k][0], he[k], "r2%d" % t, _q(T, qn, 24 * k, 24 * k + 24), _q(T, rb, 0, 24)) for k in range(2)], tk[0:1])
+        send([(hands[k][0], he[k], "r3%d" % t, T[qn + "s"][:, 24 * k:24 * k + 24], T[rb + "s"][:, 0:24]) for k in range(2)], tk)
+        cs = [12 * near.index(q) for q in nq]
+        send([(cores[q], de[k], "a1%d" % t, _q(T, qn, cs[k], cs[k] + 12), _q(T, la, a, a + 12)) for k, q in enumerate(nq)], tk)
+        send([(cores[q], de[k], "a1%d" % t, T[qn + "s"][:, cs[k]:cs[k] + 12], T[la + "s"][:, a:a + 12]) for k, q in enumerate(nq)], tk)
+        t_a1 = [arrival("a1%d" % t, 2 * (6 + n_far))] + pick(la, 2 * K, qn, K, o_p0, 16)
+        cp(NI[64:128, rf:rf + 12], NI[0:64, rf:rf + 12])
+        cp(T.lea[:, 64 * t + 8 * r:64 * t + 8 * r + 2], MS, [t_ms], free=True)
         for b in range(4):
             mm(T.pd[:, 512 * b:512 * b + M], "e", 128 * b, on, True, False, t_state, free=True)
-        cp(s_(ef, 4), EA)
-        cp(s_(ef + 4, 4), EB, deps=t_ab, free=True)
-        scan(s_(pre, 4), EB, EB, 0.0, A.add, A.max, free=True)
-        red(s_(ab, 1), T.leb[:, 8 * t + 1:8 * t + 8:2], A.add, free=True)
-        cp(s_(eg, 16), s_(ef, 8).indirect(o_eg))
-        ts(s_(wa + 1, 4), s_(pre, 4), s_(ab, 1), A.min, 0.0, A.max, free=True)
-        ts(col[10], s_(aa, 1), s_(ab, 1), A.add, float(-K), A.add, free=True)
-        scan(s_(eg + 16, 8), s_(eg, 8), s_(eg, 8), 0.0, A.add, A.max)
-        ts(s_(wa + 9, 8), s_(eg + 16, 8), col[10], A.min, 0.0, A.max)
-        tk = pick(pb, 0, la, 64, o_p2, 16, t_a1)
-        a = 12 * jo
-        nd = spread(_q(T, pb, 0, 12), _q(T, lb, a, a + 12), "a2%d" % t, _q(T, rb, 0, 12), "r2%d" % t, tk[0:1])
-        spread(T[pb + "s"][:, 0:12], T[lb + "s"][:, a:a + 12], "a2%d" % t, T[rb + "s"][:, 0:12], "r3%d" % t, tk)
-        dma("y", _q(T, lb, a, a + 12), _q(T, pb, 0, 12), "o2%d" % t, tk)
-        t_a2 = [arrival("a2%d" % t, 2 * (nd + n_far)), dma("y", T[lb + "s"][:, a:a + 12], T[pb + "s"][:, 0:12], "o2%d" % t, tk)]
-        cumul(cc + 32)
-        ts(s_(cc + 32, 5), s_(cc + 32, 5), float(K), A.add)
-        tt(T.w3[:], RHO, IOT[:, M * r:M * r + M], A.not_equal, deps=[t_rho], free=True)
-        CC, LM = s_(cc, 64), T.lml[:, 48 * t:48 * t + 48]
-        u0, u1, u2, VAL = T.w1[:, 0:48], T.w1[:, 48:96], T.w1[:, 96:144], T.w2[:, 48:96]
-        cp(u0, CC.indirect(o_lo))
-        tt(u1, CC.indirect(o_of), LM, A.add, deps=t_al, free=True)
-        ts(u2, LM, 0.0, A.is_gt, free=True)
-        tt(T.w2[:, 0:48], CC.indirect(o_hi), u0, A.subtract)
-        tt(u1, u1, u2, A.mult, free=True)
-        tt(u0, LM, T.w2[:, 0:48], A.is_le)
-        tt(VAL, u0, u1, A.mult)
-        act(T.ex[:, 0:512], VAL.indirect(u_(e0, 32)), deps=[tok("v")])
-        tk1 = tok("s")
-        act(T.ex[:, 512:1024], VAL.indirect(u_(e0 + 32, 32)))
-        tk2 = tok("s")
-        cp(T.ex[:, 1024:NN], VAL.indirect(u_(e0 + 64, 32)))
-        tt(T.w4[:], T.w3[:], T.diag[:, 0:M], A.mult, free=True)
-        tr(T.vw[:, 1024:NN], T.ex[:, 1024:NN])
-        tr(T.vw[:, 0:512], T.ex[:, 0:512], deps=[tk1], free=True)
-        tr(T.vw[:, 512:1024], T.ex[:, 512:1024], deps=[tk2], free=True)
-        tt(T.w1[:], T.vw[:].indirect(o_r), T.w4[:], A.mult)
-        scan(T.w3[:], T.rs16[:, 0:M], T.w1[:], 0.0, A.mult, A.add)
-        ts(o_c, T.w3[:, 15:M:16], -1.0, A.add, 0.0, A.max)
-        ts(s_(f12, 12), T.w3[:, 15:M:16], 0.0, A.is_gt, float(M), A.mult, free=True)
-        tt(s_(f24, 12), s_(f12, 12), s_(n_w, 12), A.add)
-        cp(o_s, s_(f24, 12))
-        tk = pick(rc, 0, lb, 2 * K, o_c, M, t_a2)
-        tb = []
-        for b in range(4):
-            mm(T.pd[:, 512 * b:512 * b + M], "e", 128 * b, rc, False, True, tk, free=(b % 2 == 1))
-            if b % 2 == 1:
-                tb.append(tok("p"))
-        for b in (0, 2):
-            op("s", lambda: S.activation(T.nt[:, b:4 * M:4], T.pd[:, 512 * b:512 * b + M], F.Copy, scale=0.5), [tb[b // 2]], free=True)
-            ts(T.nt[:, b + 1:4 * M:4], T.pd[:, 512 * b + 512:512 * b + 512 + M], 0.5, A.mult, deps=[tb[b // 2]], free=True)
-        quant(on, M, 2 * M, T.nt[:], [tok("s")])
-        t_state = pick(nx, 0, on, 2 * M, o_s, M)
         if t + 1 < R:
-            t_h = heights(t + 1, t_state)
+            mm(T.pg[:, 0:M], "ur", 128 * (t + 1), on, True, True, t_ur, free=True)
+            t_pg = tok("p")
+        RF = NI[:, rf:rf + 12]
+        ts(NI[:, 192:204], RF, 5, A.logical_shift_right)
+        cp(OU[:, r2:r2 + 24:2], RF, free=True)
+        cp(OU[:, r2 + 1:r2 + 24:2], RF, free=True)
+        cp(o_r, RF, free=True)
+        tk = tok("v")
+        act(T.m2[:], T.d32[:].indirect(u_(r2, 24)), deps=[tk], q="sx")
+        t_m2 = tok("sx")
+        RHO = T.rho[:, M * t:M * t + M]
+        act(RHO, IOT[:].indirect(o_r), deps=[tk])
+        dma("y", T.rt[0:1, M * t:M * t + M], T.rho[0:1, M * t:M * t + M], "out", [tok("s")])
+        cp(OU[:, h2:h2 + 24:2], NI[:, 192:204])
+        cp(OU[:, h2 + 1:h2 + 24:2], NI[:, 192:204], free=True)
+        tt(s_(ne, 12), RF, s_(n_o, 12), A.not_equal, free=True)
+        EA, LM = T.lea[:, 64 * t:64 * t + 64:8], T.lml[:, 48 * t:48 * t + 48]
+        scan(s_(pre, 8), EA, EA, 0.0, A.add, A.max, deps=t_aa + [t_c4], free=True)
+        red(s_(aa, 1), T.lea[:, 64 * t + 1:64 * t + 64:8], A.add, free=True)
+        ts(s_(wa + 1, 8), s_(pre, 8), s_(aa, 1), A.min, 0.0, A.max)
+        cumul(cc)
+        tt(s_(wx, 32), s_(cc, 32).indirect(o_n0), CN[:, dl:dl + 32], A.subtract)
+        cp(NI[:, 32:80], LM, deps=t_al, free=True)
+        tt(NI[:, 208:240], s_(cc, 32).indirect(o_n1), s_(wx, 32), A.subtract)
+        ts(NI[:, 80:128], NI[:, 32:80], 3, A.bitwise_and, free=True)
+        ts(NI[:, 0:32], NI[:, 208:240], 2, A.logical_shift_right)
+        ts(NI[:, 128:176], NI[:, 32:80], 2, A.logical_shift_right, free=True)
+        cp(s_(mj, 32), NI[:, 0:32])
+        tt(T.b1[:], NI[:, 80:128].indirect(o_d4), T.j4[:], A.is_equal, [t_lw], free=True)
+        scan(s_(exc + 1, 32), s_(mj, 32), CN[:, r8:r8 + 32], 0.0, A.add, A.mult)
+        tt(s_(pre + 8, 7), CN[:, stp:stp + 7], s_(mj + 8 * jo, 7), A.subtract, free=True)
+        ts(s_(pre, 7), s_(exc + 8 * jo + 1, 7), pI, A.is_le)
+        tt(s_(wx, 32), s_(exc, 32), CN[:, tb0:tb0 + 32], A.add, free=True)
+        tt(s_(pre, 7), s_(pre, 7), s_(pre + 8, 7), A.mult)
+        u0, u2, VAL = T.w1[:, 0:48], T.w1[:, 96:144], T.w2[:, 48:96]
+        tt(u2, NI[:, 208:240].indirect(o_va), LM, A.is_gt, free=True)
+        red(col[9], s_(pre, 7), A.add)
+        tt(T.b2[:], s_(wx, 32).indirect(o_tb), T.b1[:], A.mult, free=True)
+        ts(o_p2, col[9], col[15], A.add, 111.0, A.min)
+        scan(T.b1[:], T.rs4[:], T.b2[:], 0.0, A.mult, A.add, free=True)
+        tk = pick(pb, 0, la, 112, o_p2, 16, t_a1)
+        a = STEP * jo
+        ke = [e_off[0:4], e_off[4:8], e_on[0:4]]
+        send([(cores[q], ke[k], "a2%d" % t, _q(T, pb, 0, KEEP), _q(T, lb, a, a + KEEP)) for k, q in enumerate(nq)], tk[0:1])
+        send([(cores[q], ke[k], "a2%d" % t, T[pb + "s"][:, 0:KEEP], T[lb + "s"][:, a:a + KEEP]) for k, q in enumerate(nq)], tk)
+        t_a2 = [arrival("a2%d" % t, 24)] + pick(lb, a, la, 112, o_p2, 16)
+        tt(u0, T.b1[:, 3:M:4], NI[:, 128:176], A.add)
+        tt(VAL, u0, u2, A.mult)
+        tt(T.b4[:], VAL.indirect(u_(h2, 24)), T.m2[:], A.mult, deps=[t_m2])
+        tr(T.b5[:], T.b4[:])
+        scan(T.b4[:], T.rs32[:], T.b5[:], 0.0, A.mult, A.add)
+        tt(s_(ne, 12), T.b4[:, 31:384:32], s_(ne, 12), A.mult)
+        ts(o_c, s_(ne, 12), -1.0, A.add, 0.0, A.max)
+        if t + 1 < R:
+            tr(T.ho[:], T.pg[:, 0:M], deps=[t_pg], free=True)
+        tk = pick(rc, 0, lb, 4 * STEP, o_c, M, t_a2)
+        ts(s_(f12, 12), s_(ne, 12), 0.0, A.is_gt, float(M), A.mult)
+        if t + 1 < R:
+            ts(s_(m32, 16), s_(ne, 16).indirect(o_x), 0.0, A.is_gt, free=True)
+        tt(s_(f24, 12), s_(f12, 12), s_(n_w, 12), A.add)
+        if t + 1 < R:
+            ts(s_(om + 8, 6), s_(m32, 6), -1.0, A.mult, 1.0, A.add, free=True)
+        cp(o_s, s_(f24, 12))
+        if t + 1 < R:
+            tt(s_(om, 6), T.ho[:, 0:M:32], s_(om + 8, 6), A.mult, free=True)
+        wait("p", tok("p"))
+        tb = []
+        for b, q in enumerate(("p", "p1", "p2", "p3")):
+            mm(T.pd[:, 512 * b:512 * b + M], "e", 128 * b, rc, False, True, tk, free=True, q=q)
+            tb.append(tok(q))
+        for b in (0, 1):
+            op("s", lambda: S.activation(T.nt[:, b:4 * M:4], T.pd[:, 512 * b:512 * b + M], F.Copy, scale=0.5), [tb[b]], free=True)
+        for b in (2, 3):
+            ts(T.nt[:, b:4 * M:4], T.pd[:, 512 * b:512 * b + M], 0.5, A.mult, deps=[tb[b]], free=True)
+        quant(on, M, 2 * M, T.nt[:], [tok("s")])
+        if t + 1 < R:
+            mm(T.ph[:, 0:M], "ur", 128 * (t + 1), on, True, True, [tok("v")], x0=M)
+            tr(T.ht[:], T.ph[:, 0:M], deps=[tok("p")])
+            tt(s_(om + 8, 6), T.ht[:, 0:M:32], s_(m32, 6), A.mult)
+            tt(T.hs[:, 6 * t + 6:6 * t + 12], s_(om + 8, 6), s_(om, 6), A.add)
+            t_h = send_heights(t + 1)
+        t_state = pick(nx, 0, on, 2 * M, o_s, M)
+        if t + 2 < R:
+            t_ur = pick("ur", 128 * (t + 2), "u", 128, o_ut[t + 2], 128)
+        elif t + 2 == R:
+            quant("w", 0, 128, T.wt[:], [t_w])
 
     on = "on%d" % R
     mm(T.ph[:, 0:M], "w", 0, on, True, True, t_state)
@@ -644,7 +698,7 @@ def rank_program(g, core, T, topo):
         dma("s", T.osc[4 * k:4 * k + 4, 0:M], T[on + "s"][32 * k:32 * k + 4, 0:M], "out", t_state)
     cp(T.yb[:], T.ph[:, 0:M], deps=[tok("p")])
     dma("y", T.y[:], T.yb[:], "out", [tok("v")])
-    for q in "vxzspc":
+    for q in ENGINE:
         wait("c", (q, cnt[q]))
     wait("c", ("ls", sent[0]))
     for name in total:

from concourse.bass import DstId, RemoteDMATransfer
from concourse.mybir import dt, AluOpType, AxisListType, ActivationFunctionType

N, M, K, J, R = 8, 192, 48, 3, 3
NN = N * M
WIDE0 = 2
LEVELS = [(2, 2), (2, 2), (1, 1)]
TAIL = 2
FIRST_S = 56
HAND_ENG = 4
KEEP, STEP = 15, 16
C4, U8, F32, B16, I32, U16 = "float8_e4m3fn_x4", "uint8", "float32", "bfloat16", "int32", "uint16"

SCRATCH = {"pd": ("psum", [128, 2048], F32), "ph": ("psum", [128, 512], F32), "pg": ("psum", [128, 512], F32)}
for _d, _l in (
        (B16, (("xt", 768), ("ut", 512), ("wt", 512), ("et", 2048), ("nt", 768), ("ms", 200 * R), ("lea", 64 * R),
               ("lw", 6 * R), ("lml", 48 * R), ("rm", 2 * R), ("rl", 6 * R), ("d32", NN), ("rs32", 384), ("m2", 384), ("b4", 384),
               ("b5", 384), ("b1", 192), ("b2", 192), ("b3", 192), ("j4", 192), ("rs4", 192))),
        (F32, (("pf", 8), ("iot", NN), ("ta", NN), ("tb", NN), ("j16", 576), ("diag", 512), ("rs16", 576), ("fw", 512),
               ("fw2", 512), ("cw", 1664), ("sm", 1024), ("hs", 6 * R), ("hl", 64 * R), ("rh", 6 * R), ("mk", 576), ("g3", 576),
               ("g3t", 576), ("sc", 832), ("ht", 192), ("ho", 192), ("g2", 384), ("g2t", 384), ("w1", 192), ("w2", 192), ("w3", 192),
               ("sj", 384), ("rho", 192 * R), ("yb", 192), ("gy", 96), ("gyt", 96), ("cn", 136), ("nbx", 160))),
        ("float16", (("g1", 96), ("g1t", 96))),
        (I32, (("pi", 8), ("ci", 112), ("ni", 256), ("nbw", 36))),
        (U16, (("ou", 768), ("nbs", 16), ("nbl", 40), ("rn", 5)))):
    for _n, _w in _l:
        SCRATCH[_n] = ("sbuf", [128, _w], _d)
_mx = [("u", 128), ("ur", 384), ("w", 128), ("e", 512)] + [("on%d" % _t, 384) for _t in range(R + 1)]
for _t in range(R):
    _mx += [("%s%d" % (_n, _t), _w) for _n, _w in (("qa", 48), ("la", 112), ("pb", 16), ("rb", 24), ("lb", 4 * STEP), ("rc", 192))]
for _n, _w in _mx:
    SCRATCH[_n + "q"] = ("sbuf", [128, _w], C4)
    SCRATCH[_n + "s"] = ("sbuf", [128, _w], U8)

ENGINE = {"v": "v", "x": "v", "z": "v", "k": "v", "s": "s", "sx": "s", "p": "p", "p1": "p", "p2": "p", "p3": "p", "c": "c"}
SEMAPHORES = list(ENGINE) + ["ls", "dx", "du", "dw", "dn", "out", "an", "rn", "on"]
for _t in range(R):
    for _n in ("ah", "aa", "al", "a1", "a2", "rh", "rm", "rl", "r2", "r3", "oh", "ol"):
        SEMAPHORES.append("%s%d" % (_n, _t))

A = AluOpType
F = ActivationFunctionType
X = AxisListType.X


def _mask(engs):
    m = 0
    for e in engs:
        m |= 1 << e
    return m


def _plan(T, topo):
    cores = list(T.cores)
    plan = []
    for r, c in enumerate(cores):
        near = [q for q in range(N) if q == r or topo.may_write(c, cores[q])]
        far = [q for q in range(N) if q not in near]
        hands = [h for h in topo.cores_of(c) if h not in cores and topo.die(h) == topo.die(c)
                 and all(topo.may_write(h, cores[q]) for q in far)][:2]
        per = len(far) // len(hands)
        plan.append({"near": near, "far": far, "hands": [(h, far[k * per:(k + 1) * per]) for k, h in enumerate(hands)]})
    return plan


def _q(T, name, a, b):
    return T[name + "q"][:, a:b].bitcast(dt.uint8)


def _dst(topo, dst, src):
    rid, pid = topo.addr(dst, src)
    return DstId(rid=rid, pnc=pid)


def hand_program(g, core, T, topo, plan, r, dests):
    cores = list(T.cores)
    engs = topo.engines(core, cores[dests[0]])
    per = len(engs) // len(dests)
    sent = [0]

    def fwd(src, dst, sem):
        g.remote_dma_fused([RemoteDMATransfer(dst_ids=[_dst(topo, cores[d], core)], dma_engine_mask=_mask(engs[k * per:(k + 1) * per]),
                                              remote_sem=T.sem[sem], src=src[k % len(src)], dst=dst) for k, d in enumerate(dests)],
                           local_sem=T.sem.ls)
        sent[0] += per * len(dests)

    g.wait_ge(T.sem.rn, HAND_ENG)
    fwd([T.rn[:, 0:5]], T.nbl[:, 5 * r:5 * r + 5], "an")
    a = 12 * r
    for t in range(R):
        g.wait_ge(T.sem["rh%d" % t], HAND_ENG)
        fwd([T.rh[:, 6 * t:6 * t + 6]], T.hl[:, 64 * t + 6 * r:64 * t + 6 * r + 6], "ah%d" % t)
        g.wait_ge(T.sem["rm%d" % t], HAND_ENG)
        fwd([T.rm[:, 2 * t:2 * t + 2]], T.lea[:, 64 * t + 8 * r:64 * t + 8 * r + 2], "aa%d" % t)
        g.wait_ge(T.sem["rl%d" % t], HAND_ENG)
        fwd([T.rl[:, 6 * t:6 * t + 6]], T.lml[:, 48 * t + 6 * r:48 * t + 6 * r + 6], "al%d" % t)
        g.wait_ge(T.sem["r2%d" % t], HAND_ENG)
        fwd([_q(T, "rb%d" % t, 12 * k, 12 * k + 12) for k in range(2)], _q(T, "la%d" % t, a, a + 12), "a1%d" % t)
        g.wait_ge(T.sem["r3%d" % t], HAND_ENG)
        fwd([T["rb%ds" % t][:, 12 * k:12 * k + 12] for k in range(2)], T["la%ds" % t][:, a:a + 12], "a1%d" % t)
    g.wait_ge(T.sem.ls, sent[0])


def rank_program(g, core, T, topo):
    plan = _plan(T, topo)
    rank = T.rank_of(core)
    if rank is None:
        for r in range(N):
            for h, dests in plan[r]["hands"]:
                if h == core:
                    hand_program(g, core, T, topo, plan, r, dests)
        return
    cores = list(T.cores)
    r = rank
    near, far, hands = plan[r]["near"], plan[r]["far"], plan[r]["hands"]
    jo = near.index(r)
    qa = r // 2
    V, S, P, Y = g.vector, g.scalar, g.tensor, g.sync
    Q = {"v": V, "s": S, "p": P, "c": g, "y": Y}
    cnt = {q: 0 for q in ENGINE}
    force = {q: False for q in ENGINE}
    waited = {}
    total = {}

    def wait(q, tok):
        name, val = tok
        q = ENGINE.get(q, q)
        if val > waited.get((q, name), 0):
            Q[q].wait_ge(T.sem[name], val)
            waited[(q, name)] = val

    def op(q, f, deps=(), free=False):
        for d in deps:
            wait(q, d)
        if not free or force[q]:
            wait(q, (q, cnt[q]))
        force[q] = False
        f().then_inc(T.sem[q], 1)
        cnt[q] += 1

    def tok(q):
        force[q] = True
        return (q, cnt[q])

    def dma(q, out, in_, sem, deps=()):
        for d in deps:
            wait(q, d)
        Q[q].dma_start(out, in_).then_inc(T.sem[sem], 16)
        total[sem] = total.get(sem, 0) + 16
        return (sem, total[sem])

    def cp(out, in_, deps=(), free=False, q="v"):
        op(q, lambda: V.tensor_copy(out, in_), deps, free)

    def tt(out, a, b, o, deps=(), free=False):
        op("v", lambda: V.tensor_tensor(out, a, b, o), deps, free)

    def ts(out, a, s1, o1, s2=None, o2=None, deps=(), free=False):
        if o2 is None:
            op("v", lambda: V.tensor_scalar(out, a, s1, None, o1), deps, free)
        else:
            op("v", lambda: V.tensor_scalar(out, a, s1, s2, o1, o2), deps, free)

    def tr(out, in_, deps=(), free=False, q="v"):
        op(q, lambda: V.transpose(out, in_), deps, free)

    def red(out, in_, o, deps=(), free=False):
        op("v", lambda: V.tensor_reduce(out, in_, X, o), deps, free)

    def scan(out, d0, d1, init, o0, o1, deps=(), free=False):
        op("v", lambda: V.tensor_tensor_scan(out, d0, d1, init, o0, o1), deps, free)

    def mset(ap, c, deps=(), free=True):
        op("v", lambda: V.memset(ap, c), deps, free)

    def quant(name, a, b, src, deps=(), free=False):
        op("v", lambda: V.quantize_mx(T[name + "q"][:, a:b], T[name + "s"][:, a:b], src), deps, free)

    def act(out, in_, deps=(), free=False, q="s"):
        op(q, lambda: S.activation(out, in_, F.Copy), deps, free)

    def mm(out, w, a, x, start, stop, deps, free=False, x0=0, q="p"):
        op(q, lambda: P.matmul_mx(out, T[w + "q"][:, a:a + 128], T[w + "s"][:, a:a + 128], T[x + "q"][:, x0:x0 + M],
                                  T[x + "s"][:, x0:x0 + M], start, stop), deps, free)

    def iota(out, pat, base, cm, flt=True):
        if flt:
            op("c", lambda: g.iota(out, pat, base, cm, allow_small_or_imprecise_dtypes=True), free=True)
        else:
            op("c", lambda: g.iota(out, pat, base, cm), free=True)

    def pick(dst, d0, src, s1, off, n, deps=()):
        dv = list(deps) + [tok("v")]
        op("s", lambda: S.activation(T[dst + "s"][:, d0:d0 + n], T[src + "s"][:, 0:s1].indirect(off), F.Copy), dv)
        cp(T[dst + "q"][:, d0:d0 + n].bitcast(dt.uint32), T[src + "q"][:, 0:s1].bitcast(dt.uint32).indirect(off), deps)
        return [tok("v"), tok("s")]

    pos = {"sm": 0, "ou": 0}

    def take(b, n):
        a = pos[b]
        pos[b] = a + (n + 7) // 8 * 8
        return a

    def sm(n):
        return take("sm", n)

    SM, OU, IOT, NI = T.sm, T.ou, T.iot, T.ni

    def u_(a, n):
        return OU[:, a:a + n]

    def ou(n):
        return u_(take("ou", n), n)

    def s_(a, n):
        return SM[:, a:a + n]

    peer = [q for q in near if q != r and cores[q] in topo.cores_of(core)]
    offc = [q for q in near if q != r and q not in peer]
    nq = offc + peer
    e_off = topo.engines(core, cores[offc[0]])
    e_on = [e for e in topo.engines(core, cores[peer[0]]) if e not in e_off]
    n_far = len(far) * (len(topo.engines(hands[0][0], cores[far[0]])) // len(hands[0][1]))
    he, de = [e_on[0:4], e_on[4:8]], [e_off[0:2], e_off[2:4], e_off[4:6]]
    sent = [0]

    def send(items, deps):
        for d in deps:
            wait("c", d)
        g.remote_dma_fused([RemoteDMATransfer(dst_ids=[_dst(topo, c, core)], dma_engine_mask=_mask(e), remote_sem=T.sem[s], src=a, dst=b)
                            for c, e, s, a, b in items], local_sem=T.sem.ls)
        sent[0] += sum(len(it[1]) for it in items)

    def spread(src, dst, sem, hdst, hsem, deps, apart=False):
        direct = [(cores[q], de[k], sem, src, dst) for k, q in enumerate(nq)]
        handed = [(hands[k][0], he[k], hsem, src, hdst) for k in range(2)]
        if apart:
            send(handed, deps)
            send(direct, deps)
        else:
            send(handed + direct, deps)
        return 6 + n_far

    def arrival(sem, n):
        total[sem] = n
        return (sem, n)

    for k in range(4):
        t_n = dma("y" if k % 2 == 0 else "s", T.nbw[16 * k:16 * k + 16, :], T.nb[:], "dn")
    t_x = dma("y", T.xt[:], T.x[:], "dx")
    t_u = dma("s", T.ut[:], T.u[:], "du")
    t_w = dma("y", T.wt[:], T.w[:], "dw")

    iota(T.pi[:, 0:1], [[0, 1]], 0, 1, flt=False)
    t_p0 = tok("c")
    iota(IOT[:, 0:256], [[1, 256]], 0, 0)
    iota(T.j16[:, 0:96], [[0, 6], [1, 16]], 0, 0)
    t_p = tok("c")
    iota(T.ci[:, 0:96], [[1, 48], [0, 2]], 0, 0, flt=False)
    iota(T.ci[:, 96:104], [[16, 4], [0, 2]], 0, 0, flt=False)
    t_c1 = tok("c")

    PI, PF = T.pi, T.pf
    c0 = sm(24)
    col = [s_(c0 + k, 1) for k in range(24)]
    place = [0, 2, 1, 3]
    for a in range(4):
        mset(SM[32 * a:32 * a + 32, c0 + 1:c0 + 2], float(5 * place[a ^ qa]))
    ts(PI[:, 1:2], PI[:, 0:1], 15, A.bitwise_and, deps=[t_p0], free=True)
    ts(PI[:, 2:3], PI[:, 0:1], 4, A.logical_shift_right, 1, A.bitwise_and, free=True)
    ts(PI[:, 3:4], PI[:, 0:1], 5, A.logical_shift_right, free=True)
    ts(PI[:, 4:5], PI[:, 0:1], 7, A.bitwise_and, free=True)
    ts(PI[:, 5:6], PI[:, 0:1], 31, A.bitwise_and, free=True)
    ts(PI[:, 6:7], PI[:, 0:1], 2, A.logical_shift_right, 3, A.bitwise_and, free=True)
    cp(PF[:, 0:7], PI[:, 0:7])
    pP, pI, pS, pA, p8, pR, pQ = [PF[:, k:k + 1] for k in range(7)]
    ts(NI[:, 0:1], pI, col[1], A.add)
    ts(NI[:, 1:2], NI[:, 0:1], 1, A.bitwise_and)
    ts(col[0], NI[:, 0:1], pS, A.add, 2.0, A.mult, free=True)
    tt(col[0], col[0], NI[:, 1:2], A.subtract)
    o_nb = ou(1)
    ts(o_nb, col[0], 35.0, A.min)
    o_ut = [ou(8) for _ in range(R)]
    for t in range(R):
        mset(o_ut[t], t)
    cp(T.nbw[64:128, :], T.nbw[0:64, :], deps=[t_n], free=True)
    cp(T.nbs[:], T.nbw[:, 0:36].indirect(o_nb))
    t_nbs = tok("v")
    nd = spread(T.nbs[:, 0:5], T.nbl[:, 5 * r:5 * r + 5], "an", T.rn[:, 0:5], "rn", [t_nbs], apart=True)
    t_an = [arrival("an", nd), dma("y", T.nbl[:, 5 * r:5 * r + 5], T.nbs[:, 0:5], "on", [t_nbs])]

    quant("u", 0, 128, T.ut[:], [t_u])
    t_ur = pick("ur", 0, "u", 128, o_ut[0], 128)
    quant("on0", 0, M, T.xt[:], [t_x], free=True)
    t_state = [tok("v")]

    def send_heights(t):
        HS = T.hs[:, 6 * t:6 * t + 6]
        tk = tok("v")
        a = 64 * t + 6 * r
        nd = spread(HS, T.hl[:, a:a + 6], "ah%d" % t, T.rh[:, 6 * t:6 * t + 6], "rh%d" % t, [tk], apart=True)
        return [arrival("ah%d" % t, nd), dma("y", T.hl[:, a:a + 6], HS, "oh%d" % t, [tk])]

    def numbers(a, n):
        op("s", lambda: S.activation(IOT[:, a:a + n], IOT[:, 0:n], F.Identity, bias=float(a)), [t_p], free=(a != 512))

    numbers(256, 256)
    numbers(512, 512)
    tk = tok("s")
    for k in range(2):
        op("sx", lambda: S.activation(T.et[:, 1024 * k:1024 * k + 1024], IOT[:, 0:1024], F.Copy, scale=0.0), [tk], free=True)
    t_et = tok("sx")
    numbers(1024, 512)
    for a, n in ((96, 96), (192, 192), (384, 192)):
        act(T.j16[:, a:a + n], T.j16[:, 0:n], free=(a != 192))
    t_iot = tok("s")
    mm(T.ph[:, 0:M], "ur", 0, "on0", True, True, t_state + t_ur)
    tr(T.ht[:], T.ph[:, 0:M], deps=[tok("p")])
    cp(T.hs[:, 0:6], T.ht[:, 0:M:32])
    t_h = send_heights(0)

    k_n, n_f, n_w, n_o, n_id = sm(3), sm(8), sm(12), sm(12), sm(48)
    CN = T.cn
    r8, dl, tb0, ones, stp = 0, 32, 64, 96, 128
    iota(T.fw[:, 0:48], [[0, 4], [1, 12]], 0, 0)
    iota(T.fw[:, 48:84], [[6, 3], [5, 2], [1, 6]], 0, 0)
    iota(T.fw2[:, 0:36], [[6, 3], [0, 2], [1, 6]], 0, 0)
    iota(T.fw[:, 84:96], [[0, 12]], 0, 0)
    iota(T.fw[:, 96:112], [[64, 8], [16, 2]], 0, 0)
    iota(T.fw[:, 112:144], [[0, 32]], 0, 0)
    iota(T.fw[:, 144:240], [[0, 2], [1, 8], [0, 6]], 24, 0)
    iota(T.fw[:, 288:320], [[1, 16], [32, 2]], 0, 0)
    for c in range(4):
        iota(T.fw[:, 240 + 12 * c:252 + 12 * c], [[-8, 12]], M - 2 - 2 * ((c - jo) % 4), 0)
    iota(T.fw[:, 320:512], [[1, 8], [0, 6], [8, 4]], 0, 0)
    t_c2 = tok("c")
    iota(T.j4[:], [[0, 48], [1, 4]], 0, 0)
    for t in range(R):
        iota(T.hl[:, 64 * t + 48:64 * t + 64], [[0, 16]], 0, 0)
    iota(T.b4[:], [[0, 12], [1, 32]], 0, 0)
    t_c3 = tok("c")
    spot = [2 * K if q == r else 12 * q for q in range(N)]
    for q in range(N):
        turn = plan[q]["near"].index(q)
        for c in range(4):
            iota(CN[:, dl + 8 * c + q:dl + 8 * c + q + 1], [[0, 1]], 3 - (c - turn) % 4, 0)
            iota(CN[:, tb0 + 8 * c + q:tb0 + 8 * c + q + 1], [[0, 1]], STEP * c + 1 - int(c < turn), 0)
        if q + 1 < N:
            iota(CN[:, stp + q:stp + q + 1], [[0, 1]], spot[q + 1] - spot[q], 0)
    for c in range(4):
        iota(CN[:, r8 + 8 * c:r8 + 8 * c + 7], [[0, 7]], 1, 0)
        iota(CN[:, r8 + 8 * c + 7:r8 + 8 * c + 8], [[0, 1]], 0, 0)
    iota(CN[:, ones:ones + 32], [[0, 32]], 1, 0)
    t_c4 = tok("c")
    op("s", lambda: S.activation(T.rs16[:], T.j16[:], F.Sign), free=True)
    t_rs = tok("s")
    for k in range(2):
        op("s", lambda: S.activation(T.cw[:, 832 * k:832 * k + 832], IOT[:, 0:832], F.Copy, scale=0.0), free=True)
    t_zero = tok("s")
    ts(T.d32[:, 0:32], IOT[:, 0:32], pR, A.is_equal, deps=[t_p])
    tk = tok("v")
    for k in (32, 64, 128, 256, 512):
        act(T.d32[:, k:2 * k], T.d32[:, 0:k], [tk])
    act(T.d32[:, 1024:NN], T.d32[:, 0:512], free=True)
    z64, y128, t16, m24, m12, e48, f24, f12 = sm(64), sm(128), sm(128), sm(24), sm(16), sm(48), sm(24), sm(32)
    kk, ka, cc, mj, wa, exc, ne = sm(8), sm(8), sm(32), sm(32), sm(32), sm(40), sm(16)
    m32, om = sm(16), sm(16)
    mset(s_(ne, 16), 0.0)
    mset(s_(f12, 32), 0.0)
    mset(s_(wa, 40), 0.0)
    o_b, o_b2, o_own, o_n0, o_n1, o_d4 = ou(1), ou(1), ou(1), ou(2), ou(2), ou(12)
    u0_, e0 = take("ou", 8), take("ou", 96)
    o_dup = u_(u0_, 8)
    ts(col[2], pS, 32.0, A.mult, free=True)
    ts(col[3], pA, 12.0, A.mult, free=True)
    ts(col[13], pI, 11.0, A.min, 32.0, A.mult, free=True)
    ts(col[14], pS, 16.0, A.mult, free=True)
    ts(col[4], pA, 10.0, A.mult, free=True)
    ts(col[6], pR, 2.0, A.add, free=True)
    ts(col[12], pR, 2.5, A.add, -1.0, A.mult, free=True)
    ts(col[7], pA, 384.0, A.mult, pR, A.add, free=True)
    cp(u_(e0, 12), T.ci[:, 0:12], [t_c1], free=True)
    ts(o_dup, T.ci[:, 96:104], pI, A.add, free=True)
    for o, k in ((o_n0, 0), (o_n1, 1)):
        ts(o, s_(f12, 2), p8, A.add, float(k), A.add, free=(k == 1))
    ts(o_d4, IOT[:, 0:48:4], pQ, A.add, free=True)
    ts(s_(n_f, 6), IOT[:, 0:192:32], pR, A.add, 1.0 / 256, A.mult, free=True)
    ts(s_(n_w, 12), IOT[:, 0:192:16], pI, A.add, free=True)
    ts(s_(n_o, 12), s_(n_w, 12), float(M * r), A.add)
    o_p0, o_x, o_e = ou(1), ou(1), ou(12)
    ts(col[5], pI, 5.0, A.min, 2.0, A.mult, free=True)
    ts(o_e, T.ci[:, 0:12], 32.0, A.mult, 31.0, A.add, free=True)
    ts(col[15], pI, float(spot[0]), A.add, free=True)
    ts(o_p0, pI, 11.0, A.min, float(12 * jo), A.add, free=True)
    ts(o_own, pI, 11.0, A.min, col[3], A.add, free=True)
    ts(o_b2, col[13], col[14], A.add, free=True)
    ts(o_x, col[5], pS, A.add)
    cp(T.w3[:], s_(n_f, 6).indirect(u_(e0, 12)), free=True)
    for b in range(4):
        ts(T.et[:, 512 * b + b:512 * b + 512:4], IOT[:, 0:128], pP, A.is_equal, deps=[t_et], free=True)
    quant("e", 0, 512, T.et[:])
    t_state = t_state + [tok("v")]
    ts(T.diag[:], T.j16[:, 0:512], pI, A.is_equal, deps=[t_iot], free=True)
    ts(s_(n_id + 36, 12), IOT[:, 0:384:32], col[7], A.add, free=True)
    for k in range(1, 4):
        ts(T.fw2[:, 48 * k:48 * k + 36], T.fw2[:, 0:36], 5.0 * k, A.is_ge, 35.0, A.mult, deps=[t_c2], free=True)
    for k in range(1, 4):
        tt(T.fw[:, 48:84], T.fw[:, 48:84], T.fw2[:, 48 * k:48 * k + 36], A.add)
    tt(T.fw2[:], T.fw[:], T.diag[:], A.mult)
    scan(T.fw[:], T.rs16[:, 0:512], T.fw2[:], 0.0, A.mult, A.add, deps=[t_rs])
    o_m, o_nbf, o_va, o_il, o_tb = ou(3), ou(3), ou(3), ou(2), ou(12)
    force["v"] = True
    for dst, a, n in ((o_m, 0, 3), (o_va, 9, 3), (s_(k_n, 3), 15, 3), (o_il, 18, 2), (o_tb, 20, 12)):
        cp(dst, T.fw[:, 16 * a + 15:16 * (a + n):16], free=True)
    ts(o_nbf, T.fw[:, 63:96:16], col[4], A.add, free=True)
    ts(o_b, T.fw[:, 111:112], col[2], A.add, 383.0, A.min, free=True)
    x0 = 128 + M * r
    ts(T.cw[:, x0:x0 + 32], IOT[:, 0:32], pR, A.is_equal, deps=[t_zero], free=True)
    ts(T.cw[:, x0 + 32:x0 + 64], IOT[:, 0:32], pR, A.is_equal, 4096.0, A.mult, free=True)
    t_ur = pick("ur", 128, "u", 128, o_ut[1], 128)
    ts(T.rs4[:], T.j4[:], 0.0, A.is_gt, deps=[t_c3], free=True)
    ts(T.rs32[:], T.b4[:], 0.0, A.is_gt, free=True)

    NB = T.nbx
    cp(NB[:, 0:40], T.nbl[:], deps=t_an, free=True)
    cp(NB[0:64, 40:80], T.nbl[64:128, :], free=True)
    cp(NB[64:128, 40:80], T.nbl[0:64, :], free=True)
    force["v"] = True
    for a in range(4):
        cp(NB[32 * a:32 * a + 32, 80:160], NB[32 * (a ^ 1):32 * (a ^ 1) + 32, 0:80], free=True)
    cp(NI[:, 0:48], NB[:].indirect(o_nbf))
    o_nh, o_nl, o_nn = ou(36), ou(36), ou(36)
    ts(NI[:, 192:228], NI[:, 0:36], 15, A.bitwise_and)
    cp(o_nn, NI[:, 0:36], free=True)
    cp(o_nl, NI[:, 192:228])
    act(T.mk[:], T.diag[:, 0:16].indirect(o_nl), deps=[tok("v")])
    t_mk = tok("s")
    act(T.g3t[:], IOT[:].indirect(o_nn))
    t_id = tok("s")
    ts(NI[:, 48:84], NI[:, 0:36], 1024, A.bitwise_and, 4, A.logical_shift_right)
    ts(NI[:, 96:132], NI[:, 0:36], 16, A.bitwise_and, free=True)
    ts(NI[:, 144:180], NI[:, 0:36], 5, A.logical_shift_right, 31, A.bitwise_and, free=True)
    tt(NI[:, 48:84], NI[:, 48:84], NI[:, 96:132], A.add)
    tt(NI[:, 144:180], NI[:, 144:180], NI[:, 96:132], A.add, free=True)
    tt(NI[:, 48:84], NI[:, 48:84], NI[:, 144:180], A.add)
    cp(o_nh, NI[:, 48:84])

    lmin = f24
    wt_, wx, pre, aa = y128 + 32, y128 + 64, m24, m24 + 16
    o_l, o_p2, o_c, o_s, o_r = ou(3), ou(1), ou(12), ou(12), ou(12)
    a0, d0, f0, h2, r2 = take("ou", 16), take("ou", 32), take("ou", 96), take("ou", 24), take("ou", 24)
    o_a = u_(a0, 12)
    H = M // 2
    rf = 176

    def hop(tab, deps, conv):
        if conv:
            cp(u_(a0 + 6, 6), T.gyt[:, 0:H:16], q="z")
            cp(u_(a0, 6), T.g1t[:, 0:H:16], q="x")
        act(T.gy[:], tab[:].indirect(u_(a0 + 6, 6)), deps=[tok("z")] + deps)
        cp(T.g1[:], tab[:].indirect(u_(a0, 6)), deps, q="x")
        tr(T.gyt[:], T.gy[:], [tok("s")], q="z")
        tr(T.g1t[:], T.g1[:], q="x")

    def doubled(tab, deps):
        cp(u_(d0 + 12, 12), T.gyt[:, 0:H:8], q="z")
        cp(u_(d0, 12), T.g1t[:, 0:H:8], q="x")
        act(T.g2[:, 192:384], tab[:].indirect(u_(d0 + 12, 12)), deps=[tok("z")] + deps)
        cp(T.g2[:, 0:192], tab[:].indirect(u_(d0, 12)), deps, q="x")
        tr(T.g2t[:, 192:384], T.g2[:, 192:384], [tok("s")], q="z")
        tr(T.g2t[:, 0:192], T.g2[:, 0:192], q="x")

    def rebuild(tab, first, wides, ahead):
        both = [tok("x"), tok("z"), tok("v")]
        new = T.tb if tab is T.ta else T.ta

        def rep(a, d, q):
            s = OU[32 * a:32 * a + 32, d0:d0 + 24] if first else T.g2t[32 * a:32 * a + 32, 0:384:16]
            cp(OU[32 * d:32 * d + 32, f0 + 24 * a:f0 + 24 * a + 24], s, both, free=True, q=q)
        for a, d in ((0, 0), (0, 1), (1, 1), (1, 0)):
            rep(a, d, "x")
        rep(2, 2, "z")
        cp(OU[64:128, f0:f0 + 48], OU[0:64, f0:f0 + 48], q="x")
        act(new[:, 0:768], tab[:].indirect(u_(f0, 48)), deps=[tok("x")], q="sx")
        for a, d in ((2, 3), (3, 3), (3, 2)):
            rep(a, d, "z")
        if not first:
            cp(u_(a0, 16), T.g2t[:].indirect(o_b if ahead % 2 else o_b2), both, q="k")
        cp(OU[0:64, f0 + 48:f0 + 96], OU[64:128, f0 + 48:f0 + 96], q="z")
        ns = FIRST_S
        act(new[:, 768:16 * ns], tab[:].indirect(u_(f0 + 48, ns - 48)), deps=[tok("z")], free=True, q="sx")
        cp(new[:, 16 * ns:NN], tab[:].indirect(u_(f0 + ns, 96 - ns)), q="z")
        dep = [tok("sx"), tok("z"), tok("x"), tok("k")]
        for _ in range(wides - 1):
            tab, new = new, T.tb if new is T.ta else T.ta
            act(new[:, 0:768], tab[:].indirect(u_(f0, 48)), deps=dep, q="sx")
            cp(new[:, 768:NN], tab[:].indirect(u_(f0 + 48, 48)), dep, q="z")
            dep = [tok("sx"), tok("z"), tok("x"), tok("k")]
        return new, dep

    def cumul(dst):
        tr(s_(wt_, 32), s_(wa, 32))
        red(col[8], s_(wt_, 32), A.add)
        ts(s_(wx, 32), CN[:, ones:ones + 32], col[8], A.mult)
        tr(s_(dst, 32), s_(wx, 32))

    for t in range(R):
        on, nx = "on%d" % t, "on%d" % (t + 1)
        act(T.sc[:, 591:832:16], T.hl[:, 64 * t:64 * t + 48].indirect(o_own), deps=t_h + [tok("v")])
        t_oh = tok("s")
        tr(s_(z64, 64), T.hl[:, 64 * t:64 * t + 64], deps=t_h)
        cp(s_(y128, 128), s_(z64, 64).indirect(o_dup))
        tr(s_(t16, 128), s_(y128, 128))
        tt(T.g3[:], s_(t16, 128).indirect(o_nh), T.mk[:], A.mult, deps=[t_mk])
        if t == 0:
            tr(T.sc[:, 0:576], T.g3t[:], deps=[t_id], free=True)
            cp(s_(n_id, 36), T.sc[:, 0:576:16])
            ts(s_(n_id, 48), s_(n_id, 48), -1.0, A.mult, 4096.0, A.add)
        tr(T.g3t[:], T.g3[:])
        scan(T.sc[:, 0:576], T.rs16[:], T.g3t[:], 0.0, A.mult, A.add)
        tt(s_(m24, 24), T.sc[:, 15:384:16], T.sc[:, 399:768:16], A.max, deps=[t_oh])
        tt(s_(m12, 12), s_(m24, 12), s_(m24 + 12, 12), A.max)
        tt(s_(e48, 48), s_(m12, 12).indirect(o_m), T.sc[:, 15:768:16], A.is_equal)
        tt(s_(e48, 48), s_(e48, 48), s_(n_id, 48), A.mult)
        tt(s_(f24, 24), s_(e48, 24), s_(e48 + 24, 24), A.max)
        tt(s_(f12, 12), s_(f24, 12), s_(f24 + 12, 12), A.max)
        tr(s_(z64, 32), s_(f12, 32))
        ts(o_a, s_(f12, 12), -1.0, A.mult, 4096.0, A.add, free=True)
        cp(s_(y128, 64), s_(z64, 32).indirect(u_(u0_, 4)))
        tr(s_(t16, 64), s_(y128, 64))
        ts(u_(d0, 32), s_(t16, 64).indirect(o_il), -1.0, A.mult, 4096.0, A.add)
        tab, dep = rebuild(IOT, True, WIDE0, 0)
        for lv, (k, wides) in enumerate(LEVELS):
            for h in range(k):
                hop(tab, dep, h > 0)
            doubled(tab, dep)
            tab, dep = rebuild(tab, False, wides, LEVELS[lv + 1][0] if lv + 1 < len(LEVELS) else TAIL)
        for h in range(TAIL):
            hop(tab, dep, h > 0)
        doubled(tab, dep)
        o_d = u_(d0, 24)
        cp(o_d, T.g2t[:, 0:384:16], [tok("x"), tok("z")])
        tk = tok("v")
        for k in range(2):
            op("s", lambda: S.activation(T.g2[:] if k else T.sj[:], T.cw[:, 128 - 64 * k:128 - 64 * k + NN].indirect(o_d), F.Copy,
                                         accum_out=s_(kk + k, 1)), [tk], free=(k == 1))
        cp(T.g3[:, 0:384], T.cw[:, 0:NN].indirect(o_d))
        red(s_(kk + 2, 1), T.g3[:, 0:384], A.add)
        s0 = 192 * (r % 2)
        for d in (0, 1):
            cp(NI[32 * d:32 * d + 32, rf:rf + 12], T.g2t[32 * qa:32 * qa + 32, s0:s0 + 192:16], free=True)
        tt(SM[0:64, ka:ka + 3], SM[0:64, kk:kk + 3], SM[64:128, kk:kk + 3], A.add, deps=[tok("s")])
        force["v"] = True
        for d in range(4):
            tt(NI[32 * d:32 * d + 32, 0:3], SM[0:32, ka:ka + 3], SM[32:64, ka:ka + 3], A.add, free=True)
        ts(NI[:, 8:14:2], NI[:, 0:3], 4095, A.bitwise_and)
        ts(NI[:, 9:14:2], NI[:, 0:3], 12, A.logical_shift_right, free=True)
        ts(T.b1[:], NI[:, 8:14].indirect(u_(e0, 12)), 33.0, A.min)
        tr(T.b2[:], T.b1[:])
        op("s", lambda: S.activation(T.sj[:, 0:M], T.b2[:], F.Sign, bias=col[12], accum_out=col[11]), [tok("v")])
        ts(T.b3[:], T.b2[:], col[6], A.is_equal)
        CUM, MS = T.ms[:, 200 * t:200 * t + M], T.ms[:, 200 * t + M - 1:200 * t + M + 1]
        scan(CUM, T.b3[:], T.b3[:], 0.0, A.add, A.max)
        t_gt = tok("s")
        op("s", lambda: S.activation(T.ms[:, 200 * t + M:200 * t + M + 1], col[11], F.Identity, bias=float(K // N - M // 2), scale=-0.5))
        t_ms = tok("s")
        a = 64 * t + 8 * r
        nd = spread(MS, T.lea[:, a:a + 2], "aa%d" % t, T.rm[:, 2 * t:2 * t + 2], "rm%d" % t, [tok("v"), t_ms])
        t_aa = [arrival("aa%d" % t, nd)]
        ts(T.b2[:], CUM, 2.0, A.mult, col[11], A.add, deps=[t_gt])
        tt(T.b1[:], T.b2[:], T.b3[:], A.mult)
        tr(T.b2[:], T.b1[:])
        scan(T.b1[:], T.rs32[:, 0:M], T.b2[:], 0.0, A.mult, A.add)
        LW = T.lw[:, 6 * t:6 * t + 6]
        op("s", lambda: S.activation(LW, T.b1[:, 31:M:32], F.Identity, bias=float(M // 2 - 1 + jo), scale=0.5), [tok("v")])
        t_lw = tok("s")
        a = 48 * t + 6 * r
        nd = spread(LW, T.lml[:, a:a + 6], "al%d" % t, T.rl[:, 6 * t:6 * t + 6], "rl%d" % t, [t_lw])
        t_al = [arrival("al%d" % t, nd), dma("y", T.lml[:, a:a + 6], LW, "ol%d" % t, [t_lw])]
        tt(T.w2[:], T.b1[:].indirect(o_e), T.w3[:], A.add)
        tr(T.w1[:], T.w2[:])
        tk = tok("v")
        tks = []
        for c, q in enumerate(("s", "sx")):
            op(q, lambda: S.activation(T.sj[:, M * c:M * c + M], T.w1[:], F.Abs, bias=s_(k_n + c, 1)), [tk], free=True)
            tks.append(tok(q))
        ts(T.w2[:], T.w1[:], s_(k_n + 2, 1), A.add)
        op("v", lambda: V.tensor_reduce(s_(lmin + 2, 1), T.w2[:], X, A.min, apply_absolute_value=True))
        for c in range(2):
            red(s_(lmin + c, 1), T.sj[:, M * c:M * c + M], A.min, deps=[tks[c]], free=True)
        ts(o_l, s_(lmin, 3), 256.0, A.mult, float(M - 1), A.min)
        qn, la, pb, lb, rb, rc = ["%s%d" % (n, t) for n in ("qa", "la", "pb", "lb", "rb", "rc")]
        tk = pick(qn, 0, on, M, o_l, K, t_state)
        a = 12 * r
        send([(hands[k][0], he[k], "r2%d" % t, _q(T, qn, 24 * k, 24 * k + 24), _q(T, rb, 0, 24)) for k in range(2)], tk[0:1])
        send([(hands[k][0], he[k], "r3%d" % t, T[qn + "s"][:, 24 * k:24 * k + 24], T[rb + "s"][:, 0:24]) for k in range(2)], tk)
        cs = [12 * near.index(q) for q in nq]
        send([(cores[q], de[k], "a1%d" % t, _q(T, qn, cs[k], cs[k] + 12), _q(T, la, a, a + 12)) for k, q in enumerate(nq)], tk)
        send([(cores[q], de[k], "a1%d" % t, T[qn + "s"][:, cs[k]:cs[k] + 12], T[la + "s"][:, a:a + 12]) for k, q in enumerate(nq)], tk)
        t_a1 = [arrival("a1%d" % t, 2 * (6 + n_far))] + pick(la, 2 * K, qn, K, o_p0, 16)
        cp(NI[64:128, rf:rf + 12], NI[0:64, rf:rf + 12])
        cp(T.lea[:, 64 * t + 8 * r:64 * t + 8 * r + 2], MS, [t_ms], free=True)
        for b in range(4):
            mm(T.pd[:, 512 * b:512 * b + M], "e", 128 * b, on, True, False, t_state, free=True)
        if t + 1 < R:
            mm(T.pg[:, 0:M], "ur", 128 * (t + 1), on, True, True, t_ur, free=True)
            t_pg = tok("p")
        RF = NI[:, rf:rf + 12]
        ts(NI[:, 192:204], RF, 5, A.logical_shift_right)
        cp(OU[:, r2:r2 + 24:2], RF, free=True)
        cp(OU[:, r2 + 1:r2 + 24:2], RF, free=True)
        cp(o_r, RF, free=True)
        tk = tok("v")
        act(T.m2[:], T.d32[:].indirect(u_(r2, 24)), deps=[tk], q="sx")
        t_m2 = tok("sx")
        RHO = T.rho[:, M * t:M * t + M]
        act(RHO, IOT[:].indirect(o_r), deps=[tk])
        dma("y", T.rt[0:1, M * t:M * t + M], T.rho[0:1, M * t:M * t + M], "out", [tok("s")])
        cp(OU[:, h2:h2 + 24:2], NI[:, 192:204])
        cp(OU[:, h2 + 1:h2 + 24:2], NI[:, 192:204], free=True)
        tt(s_(ne, 12), RF, s_(n_o, 12), A.not_equal, free=True)
        EA, LM = T.lea[:, 64 * t:64 * t + 64:8], T.lml[:, 48 * t:48 * t + 48]
        scan(s_(pre, 8), EA, EA, 0.0, A.add, A.max, deps=t_aa + [t_c4], free=True)
        red(s_(aa, 1), T.lea[:, 64 * t + 1:64 * t + 64:8], A.add, free=True)
        ts(s_(wa + 1, 8), s_(pre, 8), s_(aa, 1), A.min, 0.0, A.max)
        cumul(cc)
        tt(s_(wx, 32), s_(cc, 32).indirect(o_n0), CN[:, dl:dl + 32], A.subtract)
        cp(NI[:, 32:80], LM, deps=t_al, free=True)
        tt(NI[:, 208:240], s_(cc, 32).indirect(o_n1), s_(wx, 32), A.subtract)
        ts(NI[:, 80:128], NI[:, 32:80], 3, A.bitwise_and, free=True)
        ts(NI[:, 0:32], NI[:, 208:240], 2, A.logical_shift_right)
        ts(NI[:, 128:176], NI[:, 32:80], 2, A.logical_shift_right, free=True)
        cp(s_(mj, 32), NI[:, 0:32])
        tt(T.b1[:], NI[:, 80:128].indirect(o_d4), T.j4[:], A.is_equal, [t_lw], free=True)
        scan(s_(exc + 1, 32), s_(mj, 32), CN[:, r8:r8 + 32], 0.0, A.add, A.mult)
        tt(s_(pre + 8, 7), CN[:, stp:stp + 7], s_(mj + 8 * jo, 7), A.subtract, free=True)
        ts(s_(pre, 7), s_(exc + 8 * jo + 1, 7), pI, A.is_le)
        tt(s_(wx, 32), s_(exc, 32), CN[:, tb0:tb0 + 32], A.add, free=True)
        tt(s_(pre, 7), s_(pre, 7), s_(pre + 8, 7), A.mult)
        u0, u2, VAL = T.w1[:, 0:48], T.w1[:, 96:144], T.w2[:, 48:96]
        tt(u2, NI[:, 208:240].indirect(o_va), LM, A.is_gt, free=True)
        red(col[9], s_(pre, 7), A.add)
        tt(T.b2[:], s_(wx, 32).indirect(o_tb), T.b1[:], A.mult, free=True)
        ts(o_p2, col[9], col[15], A.add, 111.0, A.min)
        scan(T.b1[:], T.rs4[:], T.b2[:], 0.0, A.mult, A.add, free=True)
        tk = pick(pb, 0, la, 112, o_p2, 16, t_a1)
        a = STEP * jo
        ke = [e_off[0:4], e_off[4:8], e_on[0:4]]
        send([(cores[q], ke[k], "a2%d" % t, _q(T, pb, 0, KEEP), _q(T, lb, a, a + KEEP)) for k, q in enumerate(nq)], tk[0:1])
        send([(cores[q], ke[k], "a2%d" % t, T[pb + "s"][:, 0:KEEP], T[lb + "s"][:, a:a + KEEP]) for k, q in enumerate(nq)], tk)
        t_a2 = [arrival("a2%d" % t, 24)] + pick(lb, a, la, 112, o_p2, 16)
        tt(u0, T.b1[:, 3:M:4], NI[:, 128:176], A.add)
        tt(VAL, u0, u2, A.mult)
        tt(T.b4[:], VAL.indirect(u_(h2, 24)), T.m2[:], A.mult, deps=[t_m2])
        tr(T.b5[:], T.b4[:])
        scan(T.b4[:], T.rs32[:], T.b5[:], 0.0, A.mult, A.add)
        tt(s_(ne, 12), T.b4[:, 31:384:32], s_(ne, 12), A.mult)
        ts(o_c, s_(ne, 12), -1.0, A.add, 0.0, A.max)
        if t + 1 < R:
            tr(T.ho[:], T.pg[:, 0:M], deps=[t_pg], free=True)
        tk = pick(rc, 0, lb, 4 * STEP, o_c, M, t_a2)
        ts(s_(f12, 12), s_(ne, 12), 0.0, A.is_gt, float(M), A.mult)
        if t + 1 < R:
            ts(s_(m32, 16), s_(ne, 16).indirect(o_x), 0.0, A.is_gt, free=True)
        tt(s_(f24, 12), s_(f12, 12), s_(n_w, 12), A.add)
        if t + 1 < R:
            ts(s_(om + 8, 6), s_(m32, 6), -1.0, A.mult, 1.0, A.add, free=True)
        cp(o_s, s_(f24, 12))
        if t + 1 < R:
            tt(s_(om, 6), T.ho[:, 0:M:32], s_(om + 8, 6), A.mult, free=True)
        wait("p", tok("p"))
        tb = []
        for b, q in enumerate(("p", "p1", "p2", "p3")):
            mm(T.pd[:, 512 * b:512 * b + M], "e", 128 * b, rc, False, True, tk, free=True, q=q)
            tb.append(tok(q))
        for b in (0, 1):
            op("s", lambda: S.activation(T.nt[:, b:4 * M:4], T.pd[:, 512 * b:512 * b + M], F.Copy, scale=0.5), [tb[b]], free=True)
        for b in (2, 3):
            ts(T.nt[:, b:4 * M:4], T.pd[:, 512 * b:512 * b + M], 0.5, A.mult, deps=[tb[b]], free=True)
        quant(on, M, 2 * M, T.nt[:], [tok("s")])
        if t + 1 < R:
            mm(T.ph[:, 0:M], "ur", 128 * (t + 1), on, True, True, [tok("v")], x0=M)
            tr(T.ht[:], T.ph[:, 0:M], deps=[tok("p")])
            tt(s_(om + 8, 6), T.ht[:, 0:M:32], s_(m32, 6), A.mult)
            tt(T.hs[:, 6 * t + 6:6 * t + 12], s_(om + 8, 6), s_(om, 6), A.add)
            t_h = send_heights(t + 1)
        t_state = pick(nx, 0, on, 2 * M, o_s, M)
        if t + 2 < R:
            t_ur = pick("ur", 128 * (t + 2), "u", 128, o_ut[t + 2], 128)
        elif t + 2 == R:
            quant("w", 0, 128, T.wt[:], [t_w])

    on = "on%d" % R
    mm(T.ph[:, 0:M], "w", 0, on, True, True, t_state)
    dma("y", T.oc[:, 0:4 * M], _q(T, on, 0, M), "out", t_state)
    for k in range(4):
        dma("s", T.osc[4 * k:4 * k + 4, 0:M], T[on + "s"][32 * k:32 * k + 4, 0:M], "out", t_state)
    cp(T.yb[:], T.ph[:, 0:M], deps=[tok("p")])
    dma("y", T.y[:], T.yb[:], "out", [tok("v")])
    for q in ENGINE:
        wait("c", (q, cnt[q]))
    wait("c", ("ls", sent[0]))
    for name in total:
        wait("c", (name, total[name]))
